import numpy as np
import ml_dtypes


def mxq(x, axis, fmt="e4m3"):
    dtype, down = {"e4m3": (ml_dtypes.float8_e4m3fn, 7), "e5m2": (ml_dtypes.float8_e5m2, 14)}[fmt]
    v = np.moveaxis(np.asarray(x, np.float32).astype(ml_dtypes.bfloat16).astype(np.float64), axis, -1)
    blocks = v.reshape(v.shape[:-1] + (-1, 32))
    amax = np.abs(blocks).max(-1, keepdims=True)
    byte = np.maximum(np.where(amax > 0, np.frexp(amax)[1] - 1 + 127, 0) - down, 1)
    scale = np.exp2(byte - 127.0)
    codes = (blocks / scale).astype(np.float32).astype(dtype).astype(np.float64)
    return np.moveaxis((codes * scale).reshape(v.shape), -1, axis)


WIDE = False


def mx_kscale(k):
    if not WIDE:
        return np.ones(k)
    levels = np.array([10, -10, 5, -5, 0])
    if k % 512:
        return np.exp2(np.random.permutation(np.resize(levels, k // 32))).repeat(32)
    a = np.empty((k // 512, 16))
    for p in range(k // 512):
        a[p, :8] = np.random.permutation(np.resize(levels, 8))
        for g in range(8):
            far = levels[np.abs(levels - a[p, g]) >= 10]
            a[p, g + 8] = far[np.random.randint(len(far))]
    return np.exp2(a.ravel()).repeat(32)


def f64(x):
    return np.asarray(x).astype(np.float64)


def striped(idx):
    return np.tile(idx.reshape(-1, 16).T, (8, 1)).astype(np.uint16)


def unstriped(offs):
    return offs[:16].T.reshape(-1).astype(np.int64)

def planes(y):
    n, m = y.shape
    v = y.astype(np.float32).astype(ml_dtypes.bfloat16).astype(np.float64).reshape(n // 32, 32, m)
    top = np.abs(v).max(1)
    byte = np.clip(np.where(top > 0, np.frexp(top)[1] - 1 + 127 - 7, 1), 1, 254)
    codes = (v * np.exp2(127.0 - byte)[:, None, :]).reshape(n, m).astype(np.float32).astype(ml_dtypes.float8_e4m3fn).view(np.uint8)
    words = codes.reshape(n // 512, 128, 4, m).transpose(0, 1, 3, 2)
    return np.ascontiguousarray(words), np.ascontiguousarray(byte.astype(np.uint8).reshape(n // 512, 16, m))


K, T, S, V, N = 512, 1024, 512, 256, 512
P = 2 ** 7


def setup_inputs():
    n = np.random.standard_normal
    s = mx_kscale(K)[:, None]
    return {
        "xT": (n((K, T)) * s).astype(np.float32),
        "w1": (n((K, N)) / np.sqrt(K) / s).astype(np.float32),
        "frac": np.tile(np.random.uniform(0.05, 0.95, V), (P, 1)).astype(np.float32),
        "offs": striped(np.random.permutation(T)[:S]),
        "left": striped(np.random.permutation(S)[:V]),
        "right": striped(np.random.permutation(S)[:V]),
    }


def reference(xT, w1, frac, offs, left, right):
    xq = mxq(f64(xT)[:, unstriped(offs)], 0, "e4m3")
    y = mxq(f64(w1), 0, "e4m3").T @ xq
    l = y[:, unstriped(left)]
    out_0 = l + (y[:, unstriped(right)] - l) * f64(frac)[:1]
    return (out_0,) + planes(out_0)

@@ -1,0 +1,210 @@
+from contextlib import ExitStack
+
+import concourse.mybir as mybir
+
+K, T, S, V, N = 512, 1024, 512, 256, 512
+FLOPS = 2 * K * N * S
+
+F32 = mybir.dt.float32
+BF16 = mybir.dt.bfloat16
+I32 = mybir.dt.int32
+U32 = mybir.dt.uint32
+U16 = mybir.dt.uint16
+U8 = mybir.dt.uint8
+FP8X4 = mybir.dt.float8_e4m3fn_x4
+MULT = mybir.AluOpType.mult
+ADD = mybir.AluOpType.add
+IDENTITY = mybir.ActivationFunctionType.Identity
+
+P = 128
+PACK = 4
+HALF_T = T // 2
+HALF_S = S // 2
+HALF_N = N // 2
+HALF_V = V // 2
+X_TAIL_SCALAR = 176
+W_TAIL_SCALAR = 40
+
+
+def tile_picked_lerp_none_lo_kernel(
+    tc, xT, w1, frac, offs, left, right, out_0, out_1, out_2
+):
+    nc = tc.nc
+    with ExitStack() as ctx:
+        lists = ctx.enter_context(tc.tile_pool(name="lists", bufs=1))
+        pool = ctx.enter_context(tc.tile_pool(name="pool", bufs=1))
+        psum = ctx.enter_context(tc.psum_pool(name="psum", bufs=1))
+
+        offs_sb = lists.tile([P, S // 16], U16, name="offs_sb")
+        left_sb = lists.tile([P, V // 16], U16, name="left_sb")
+        right_sb = lists.tile([P, V // 16], U16, name="right_sb")
+
+        x_rows = xT.rearrange("(p j) t -> p j t", j=PACK)
+        w_rows = w1.rearrange("(p j) m -> p j m", j=PACK)
+        x_raw = [[pool.tile([P, 2, HALF_T], F32, name=f"x_raw{u}{h}") for h in range(2)] for u in range(2)]
+        w_raw = [pool.tile([P, PACK, HALF_N], F32, name=f"w_raw{h}") for h in range(2)]
+        frac_sb = pool.tile([P, V], F32, name="frac_sb")
+
+        def load_x(u, h):
+            nc.sync.dma_start(out=x_raw[u][h][:], in_=x_rows[:, 2 * u : 2 * u + 2, h * HALF_T : (h + 1) * HALF_T])
+
+        load_x(0, 0)
+        load_x(0, 1)
+        nc.sync.dma_start(offs_sb[:], offs)
+        load_x(1, 0)
+        load_x(1, 1)
+        for h in range(2):
+            nc.sync.dma_start(out=w_raw[h][:], in_=w_rows[:, :, h * HALF_N : (h + 1) * HALF_N])
+        nc.sync.dma_start(out=frac_sb[:], in_=frac)
+        nc.sync.dma_start(left_sb[:], left)
+        nc.sync.dma_start(right_sb[:], right)
+
+        one_src = pool.tile([P, 1], F32, name="one_src")
+        one = pool.tile([P, 1], F32, name="one")
+        nc.gpsimd.memset(one_src[:], 1.0)
+        nc.scalar.copy(out=one[:], in_=one_src[:])
+
+        x_pairs = [pool.tile([P, T, 2], BF16, name=f"x_pairs{u}") for u in range(2)]
+        x_picked = [pool.tile([P, HALF_S, PACK], BF16, name=f"x_picked{h}", align_bytes=64) for h in range(2)]
+        x_codes = pool.tile([P, S], U32, name="x_codes", align_bytes=64)
+        x_scales = pool.tile([P, S], U8, name="x_scales", align_bytes=64)
+
+        def pair_views(u, h, c0, c1):
+            dst = x_pairs[u][:, h * HALF_T + c0 : h * HALF_T + c1, :]
+            src = x_raw[u][h][:, :, c0:c1].rearrange("p j c -> p c j")
+            return dst, src
+
+        def gather_x(u, h):
+            window = x_pairs[u][:].rearrange("p c j -> p (c j)").bitcast(U32)
+            words = x_picked[h][:].rearrange("p s j -> p (s j)").bitcast(U32).rearrange("p (s u) -> p s u", u=2)
+            cols = HALF_S // 16
+            nc.vector.tensor_copy(out=words[:, :, u], in_=window.indirect(offs_sb[:, h * cols : (h + 1) * cols]))
+
+        nc.scalar.copy(*pair_views(0, 0, 0, HALF_T))
+        nc.vector.tensor_copy(*pair_views(0, 1, 0, HALF_T))
+        gather_x(0, 0)
+        gather_x(0, 1)
+        nc.scalar.copy(*pair_views(1, 0, 0, HALF_T))
+        nc.scalar.copy(*pair_views(1, 1, 0, X_TAIL_SCALAR))
+        nc.vector.tensor_copy(*pair_views(1, 1, X_TAIL_SCALAR, HALF_T))
+        gather_x(1, 0)
+        gather_x(1, 1)
+        for h in range(2):
+            cols = slice(h * HALF_S, (h + 1) * HALF_S)
+            nc.vector.quantize_mx(
+                out=x_codes[:, cols].bitcast(FP8X4),
+                scales=x_scales[:, cols],
+                in_=x_picked[h][:].rearrange("p s j -> p (s j)"),
+            )
+
+        w_dealt = pool.tile([P, PACK, P, PACK], BF16, name="w_dealt", align_bytes=64)
+        w_codes = pool.tile([P, N], U32, name="w_codes", align_bytes=64)
+        w_scales = pool.tile([P, N], U8, name="w_scales", align_bytes=64)
+        half_m = P // 2
+
+        def deal_views(h, m0, m1):
+            dst = w_dealt[:, :, h * half_m + m0 : h * half_m + m1, :].rearrange("p t m j -> p m j t")
+            src = w_raw[h][:, :, PACK * m0 : PACK * m1].rearrange("p j (m t) -> p m j t", t=PACK)
+            return dst, src
+
+        nc.scalar.copy(*deal_views(0, 0, half_m))
+        nc.scalar.copy(*deal_views(1, 0, W_TAIL_SCALAR))
+        nc.vector.tensor_copy(*deal_views(1, W_TAIL_SCALAR, half_m))
+        for t in range(PACK):
+            cols = slice(t * P, (t + 1) * P)
+            nc.vector.quantize_mx(
+                out=w_codes[:, cols].bitcast(FP8X4),
+                scales=w_scales[:, cols],
+                in_=w_dealt[:, t, :, :].rearrange("p m j -> p (m j)"),
+            )
+
+        rest_sb = pool.tile([P, V], F32, name="rest_sb")
+        nc.scalar.activation(out=rest_sb[:], in_=frac_sb[:], func=IDENTITY, bias=one[:], scale=-1.0)
+
+        y = [pool.tile([P, S], F32, name=f"y{t}") for t in range(PACK)]
+
+        def product(t, acc, cols):
+            rows = slice(t * P, (t + 1) * P)
+            nc.tensor.matmul_mx(
+                out=acc,
+                lhsT=w_codes[:, rows].bitcast(FP8X4),
+                lhsT_scale=w_scales[:, rows],
+                rhs=x_codes[:, cols].bitcast(FP8X4),
+                rhs_scale=x_scales[:, cols],
+                start=True,
+                stop=True,
+            )
+
+        first = [psum.tile([P, HALF_S], F32, name=f"first{h}") for h in range(2)]
+        for h in range(2):
+            product(0, first[h][:], slice(h * HALF_S, (h + 1) * HALF_S))
+        nc.scalar.copy(out=y[0][:, :HALF_S], in_=first[0][:])
+        nc.vector.tensor_copy(out=y[0][:, HALF_S:], in_=first[1][:])
+        for t in range(1, PACK):
+            acc = psum.tile([P, S], F32, name=f"acc{t}")
+            product(t, acc[:], slice(0, S))
+            nc.scalar.copy(out=y[t][:], in_=acc[:])
+
+        last = PACK - 1
+        left_part = pool.tile([P, last, V], F32, name="left_part")
+        right_part = pool.tile([P, last, V], F32, name="right_part")
+        left_last = [pool.tile([P, HALF_V], F32, name=f"left_last{h}") for h in range(2)]
+        right_last = [pool.tile([P, HALF_V], F32, name=f"right_last{h}") for h in range(2)]
+        result = [pool.tile([P, PACK, HALF_V], F32, name=f"result{h}") for h in range(2)]
+        rounded = [pool.tile([P, HALF_V, PACK], BF16, name=f"rounded{h}", align_bytes=64) for h in range(2)]
+        o_codes = pool.tile([P, V], U32, name="o_codes", align_bytes=64)
+        o_scales = pool.tile([P, V], U8, name="o_scales", align_bytes=64)
+        out_rows = out_0.rearrange("(p t) v -> p t v", t=PACK)
+
+        for t in range(last):
+            nc.vector.tensor_tensor(left_part[:, t, :], y[t][:].indirect(left_sb[:]), rest_sb[:], MULT)
+            nc.vector.tensor_tensor(right_part[:, t, :], y[t][:].indirect(right_sb[:]), frac_sb[:], MULT)
+
+        def v_cols(h):
+            return slice(h * HALF_V, (h + 1) * HALF_V)
+
+        def gather_last(dst, places, factor, h):
+            cols = HALF_V // 16
+            nc.vector.tensor_tensor(
+                dst[h][:], y[last][:].indirect(places[:, h * cols : (h + 1) * cols]), factor[:, v_cols(h)], MULT
+            )
+
+        def add_early(h):
+            nc.vector.tensor_tensor(result[h][:, :last, :], left_part[:, :, v_cols(h)], right_part[:, :, v_cols(h)], ADD)
+            nc.sync.dma_start(out=out_rows[:, :last, v_cols(h)], in_=result[h][:, :last, :])
+
+        def add_last(h):
+            nc.vector.tensor_tensor(result[h][:, last, :], left_last[h][:], right_last[h][:], ADD)
+            nc.sync.dma_start(out=out_rows[:, last, v_cols(h)], in_=result[h][:, last, :])
+
+        def round_views(h):
+            return rounded[h][:], result[h][:].rearrange("p t v -> p v t")
+
+        def quantize_result(h):
+            nc.vector.quantize_mx(
+                out=o_codes[:, v_cols(h)].bitcast(FP8X4),
+                scales=o_scales[:, v_cols(h)],
+                in_=rounded[h][:].rearrange("p v t -> p (v t)"),
+            )
+
+        gather_last(left_last, left_sb, rest_sb, 0)
+        add_early(0)
+        gather_last(right_last, right_sb, frac_sb, 0)
+        gather_last(left_last, left_sb, rest_sb, 1)
+        add_last(0)
+        nc.scalar.copy(*round_views(0))
+        gather_last(right_last, right_sb, frac_sb, 1)
+        add_early(1)
+        add_last(1)
+        quantize_result(0)
+        nc.vector.tensor_copy(*round_views(1))
+        quantize_result(1)
+
+        nc.sync.dma_start(
+            out=out_1.rearrange("z p c r -> p (z c r)").bitcast(I32), in_=o_codes[:].bitcast(I32)
+        )
+        for q in range(4):
+            queue = nc.scalar if q % 2 == 0 else nc.sync
+            queue.dma_start(
+                out=out_2[0, 4 * q : 4 * q + 4, :].bitcast(I32), in_=o_scales[32 * q : 32 * q + 4, :].bitcast(I32)
+            )

@@ -18,12 +18,9 @@ IDENTITY = mybir.ActivationFunctionType.Identity
 
 P = 128
 PACK = 4
-HALF_T = T // 2
 HALF_S = S // 2
 HALF_N = N // 2
 HALF_V = V // 2
-X_TAIL_SCALAR = 176
-W_TAIL_SCALAR = 40
 
 
 def tile_picked_lerp_none_lo_kernel(
@@ -41,18 +38,14 @@ def tile_picked_lerp_none_lo_kernel(
 
         x_rows = xT.rearrange("(p j) t -> p j t", j=PACK)
         w_rows = w1.rearrange("(p j) m -> p j m", j=PACK)
-        x_raw = [[pool.tile([P, 2, HALF_T], F32, name=f"x_raw{u}{h}") for h in range(2)] for u in range(2)]
+        x_raw = [pool.tile([P, T], F32, name=f"x_raw{j}") for j in range(PACK)]
         w_raw = [pool.tile([P, PACK, HALF_N], F32, name=f"w_raw{h}") for h in range(2)]
         frac_sb = pool.tile([P, V], F32, name="frac_sb")
 
-        def load_x(u, h):
-            nc.sync.dma_start(out=x_raw[u][h][:], in_=x_rows[:, 2 * u : 2 * u + 2, h * HALF_T : (h + 1) * HALF_T])
-
-        load_x(0, 0)
-        load_x(0, 1)
+        nc.sync.dma_start(out=x_raw[0][:], in_=x_rows[:, 0, :])
         nc.sync.dma_start(offs_sb[:], offs)
-        load_x(1, 0)
-        load_x(1, 1)
+        for j in range(1, PACK):
+            nc.sync.dma_start(out=x_raw[j][:], in_=x_rows[:, j, :])
         for h in range(2):
             nc.sync.dma_start(out=w_raw[h][:], in_=w_rows[:, :, h * HALF_N : (h + 1) * HALF_N])
         nc.sync.dma_start(out=frac_sb[:], in_=frac)
@@ -64,32 +57,31 @@ def tile_picked_lerp_none_lo_kernel(
         nc.gpsimd.memset(one_src[:], 1.0)
         nc.scalar.copy(out=one[:], in_=one_src[:])
 
-        x_pairs = [pool.tile([P, T, 2], BF16, name=f"x_pairs{u}") for u in range(2)]
+        x_found = [pool.tile([P, 2, S], F32, name=f"x_found{u}") for u in range(2)]
         x_picked = [pool.tile([P, HALF_S, PACK], BF16, name=f"x_picked{h}", align_bytes=64) for h in range(2)]
         x_codes = pool.tile([P, S], U32, name="x_codes", align_bytes=64)
         x_scales = pool.tile([P, S], U8, name="x_scales", align_bytes=64)
 
-        def pair_views(u, h, c0, c1):
-            dst = x_pairs[u][:, h * HALF_T + c0 : h * HALF_T + c1, :]
-            src = x_raw[u][h][:, :, c0:c1].rearrange("p j c -> p c j")
+        def weave_views(u, h):
+            dst = x_picked[h][:, :, 2 * u : 2 * u + 2]
+            src = x_found[u][:, :, h * HALF_S : (h + 1) * HALF_S].rearrange("p j s -> p s j")
             return dst, src
 
-        def gather_x(u, h):
-            window = x_pairs[u][:].rearrange("p c j -> p (c j)").bitcast(U32)
-            words = x_picked[h][:].rearrange("p s j -> p (s j)").bitcast(U32).rearrange("p (s u) -> p s u", u=2)
-            cols = HALF_S // 16
-            nc.vector.tensor_copy(out=words[:, :, u], in_=window.indirect(offs_sb[:, h * cols : (h + 1) * cols]))
-
-        nc.scalar.copy(*pair_views(0, 0, 0, HALF_T))
-        nc.vector.tensor_copy(*pair_views(0, 1, 0, HALF_T))
-        gather_x(0, 0)
-        gather_x(0, 1)
-        nc.scalar.copy(*pair_views(1, 0, 0, HALF_T))
-        nc.scalar.copy(*pair_views(1, 1, 0, X_TAIL_SCALAR))
-        nc.vector.tensor_copy(*pair_views(1, 1, X_TAIL_SCALAR, HALF_T))
-        gather_x(1, 0)
-        gather_x(1, 1)
+        for j in range(PACK - 1):
+            nc.vector.tensor_copy(out=x_found[j // 2][:, j % 2, :], in_=x_raw[j][:].indirect(offs_sb[:]))
+            if j == 1:
+                for h in range(2):
+                    nc.scalar.copy(*weave_views(0, h))
         for h in range(2):
+            cols = HALF_S // 16
+            nc.vector.tensor_copy(
+                out=x_found[1][:, 1, h * HALF_S : (h + 1) * HALF_S],
+                in_=x_raw[PACK - 1][:].indirect(offs_sb[:, h * cols : (h + 1) * cols]),
+            )
+        for h in range(2):
+            nc.vector.tensor_copy(*weave_views(1, h))
+
+        def quantize_x(h):
             cols = slice(h * HALF_S, (h + 1) * HALF_S)
             nc.vector.quantize_mx(
                 out=x_codes[:, cols].bitcast(FP8X4),
@@ -97,26 +89,35 @@ def tile_picked_lerp_none_lo_kernel(
                 in_=x_picked[h][:].rearrange("p s j -> p (s j)"),
             )
 
-        w_dealt = pool.tile([P, PACK, P, PACK], BF16, name="w_dealt", align_bytes=64)
         w_codes = pool.tile([P, N], U32, name="w_codes", align_bytes=64)
         w_scales = pool.tile([P, N], U8, name="w_scales", align_bytes=64)
         half_m = P // 2
 
-        def deal_views(h, m0, m1):
-            dst = w_dealt[:, :, h * half_m + m0 : h * half_m + m1, :].rearrange("p t m j -> p m j t")
-            src = w_raw[h][:, :, PACK * m0 : PACK * m1].rearrange("p j (m t) -> p m j t", t=PACK)
-            return dst, src
+        def deal_source(u, h):
+            return w_raw[h][:].rearrange("p j (m t) -> p m j t", t=PACK)[:, :, :, 2 * u : 2 * u + 2]
 
-        nc.scalar.copy(*deal_views(0, 0, half_m))
-        nc.scalar.copy(*deal_views(1, 0, W_TAIL_SCALAR))
-        nc.vector.tensor_copy(*deal_views(1, W_TAIL_SCALAR, half_m))
-        for t in range(PACK):
-            cols = slice(t * P, (t + 1) * P)
+        def quantize_w(src, c0, width):
             nc.vector.quantize_mx(
-                out=w_codes[:, cols].bitcast(FP8X4),
-                scales=w_scales[:, cols],
-                in_=w_dealt[:, t, :, :].rearrange("p m j -> p (m j)"),
+                out=w_codes[:, c0 : c0 + width].bitcast(FP8X4),
+                scales=w_scales[:, c0 : c0 + width],
+                in_=src.rearrange("p m j -> p (m j)"),
             )
+
+        w_front = pool.tile([P, 2, P, PACK], BF16, name="w_front", tag="w_dealt", align_bytes=64)
+        w_back1 = pool.tile([P, 2, half_m, PACK], BF16, name="w_back1", align_bytes=64)
+        for h in range(2):
+            dst = w_front[:, :, h * half_m : (h + 1) * half_m, :]
+            nc.scalar.copy(out=dst.rearrange("p t m j -> p m j t"), in_=deal_source(0, h))
+        nc.scalar.copy(out=w_back1[:].rearrange("p t m j -> p m j t"), in_=deal_source(1, 1))
+        quantize_x(0)
+        quantize_w(w_front[:, 0, :, :], 0, P)
+        quantize_x(1)
+        quantize_w(w_front[:, 1, :, :], P, P)
+        w_back0 = pool.tile([P, 2, half_m, PACK], BF16, name="w_back0", tag="w_dealt", align_bytes=64)
+        nc.vector.tensor_copy(out=w_back0[:].rearrange("p t m j -> p m j t"), in_=deal_source(1, 0))
+        for h, back in ((1, w_back1), (0, w_back0)):
+            for t in (2, 3):
+                quantize_w(back[:, t - 2, :, :], t * P + h * half_m, half_m)
 
         rest_sb = pool.tile([P, V], F32, name="rest_sb")
         nc.scalar.activation(out=rest_sb[:], in_=frac_sb[:], func=IDENTITY, bias=one[:], scale=-1.0)
@@ -138,8 +139,8 @@ def tile_picked_lerp_none_lo_kernel(
         first = [psum.tile([P, HALF_S], F32, name=f"first{h}") for h in range(2)]
         for h in range(2):
             product(0, first[h][:], slice(h * HALF_S, (h + 1) * HALF_S))
-        nc.scalar.copy(out=y[0][:, :HALF_S], in_=first[0][:])
-        nc.vector.tensor_copy(out=y[0][:, HALF_S:], in_=first[1][:])
+        for h in range(2):
+            nc.scalar.copy(out=y[0][:, h * HALF_S : (h + 1) * HALF_S], in_=first[h][:])
         for t in range(1, PACK):
             acc = psum.tile([P, S], F32, name=f"acc{t}")
             product(t, acc[:], slice(0, S))

@@ -1,6 +1,7 @@
 from contextlib import ExitStack
 
 import concourse.mybir as mybir
+from concourse.masks import make_identity
 
 K, T, S, V, N = 512, 1024, 512, 256, 512
 FLOPS = 2 * K * N * S
@@ -14,7 +15,7 @@ U8 = mybir.dt.uint8
 FP8X4 = mybir.dt.float8_e4m3fn_x4
 MULT = mybir.AluOpType.mult
 ADD = mybir.AluOpType.add
-IDENTITY = mybir.ActivationFunctionType.Identity
+COPY = mybir.ActivationFunctionType.Copy
 
 P = 128
 PACK = 4
@@ -30,6 +31,7 @@ def tile_picked_lerp_none_lo_kernel(
     with ExitStack() as ctx:
         lists = ctx.enter_context(tc.tile_pool(name="lists", bufs=1))
         pool = ctx.enter_context(tc.tile_pool(name="pool", bufs=1))
+        reused = ctx.enter_context(tc.tile_pool(name="reused", bufs=1))
         psum = ctx.enter_context(tc.psum_pool(name="psum", bufs=1))
 
         offs_sb = lists.tile([P, S // 16], U16, name="offs_sb")
@@ -49,13 +51,17 @@ def tile_picked_lerp_none_lo_kernel(
         for h in range(2):
             nc.sync.dma_start(out=w_raw[h][:], in_=w_rows[:, :, h * HALF_N : (h + 1) * HALF_N])
         nc.sync.dma_start(out=frac_sb[:], in_=frac)
-        nc.sync.dma_start(left_sb[:], left)
         nc.sync.dma_start(right_sb[:], right)
+        nc.sync.dma_start(left_sb[:], left)
 
-        one_src = pool.tile([P, 1], F32, name="one_src")
-        one = pool.tile([P, 1], F32, name="one")
-        nc.gpsimd.memset(one_src[:], 1.0)
-        nc.scalar.copy(out=one[:], in_=one_src[:])
+        frac_col = pool.tile([P, 2], F32, name="frac_col")
+        rest_col = pool.tile([P, 2], F32, name="rest_col")
+        with nc.allow_non_contiguous_dma(reason="one value of frac a partition"):
+            nc.sync.dma_start(out=frac_col[:], in_=frac[0, :].rearrange("(h p) -> p h", p=P))
+        nc.scalar.activation(out=rest_col[:], in_=frac_col[:], func=COPY, bias=1.0, scale=-1.0)
+
+        identity = pool.tile([P, P], F32, name="identity")
+        make_identity(nc, identity[:])
 
         x_found = [pool.tile([P, 2, S], F32, name=f"x_found{u}") for u in range(2)]
         x_picked = [pool.tile([P, HALF_S, PACK], BF16, name=f"x_picked{h}", align_bytes=64) for h in range(2)]
@@ -103,7 +109,7 @@ def tile_picked_lerp_none_lo_kernel(
                 in_=src.rearrange("p m j -> p (m j)"),
             )
 
-        w_front = pool.tile([P, 2, P, PACK], BF16, name="w_front", tag="w_dealt", align_bytes=64)
+        w_front = reused.tile([P, 2, P, PACK], BF16, name="w_front", align_bytes=64, offset=0)
         w_back1 = pool.tile([P, 2, half_m, PACK], BF16, name="w_back1", align_bytes=64)
         for h in range(2):
             dst = w_front[:, :, h * half_m : (h + 1) * half_m, :]
@@ -113,14 +119,15 @@ def tile_picked_lerp_none_lo_kernel(
         quantize_w(w_front[:, 0, :, :], 0, P)
         quantize_x(1)
         quantize_w(w_front[:, 1, :, :], P, P)
-        w_back0 = pool.tile([P, 2, half_m, PACK], BF16, name="w_back0", tag="w_dealt", align_bytes=64)
+        w_back0 = reused.tile([P, 2, half_m, PACK], BF16, name="w_back0", align_bytes=64, offset=0)
         nc.vector.tensor_copy(out=w_back0[:].rearrange("p t m j -> p m j t"), in_=deal_source(1, 0))
         for h, back in ((1, w_back1), (0, w_back0)):
             for t in (2, 3):
                 quantize_w(back[:, t - 2, :, :], t * P + h * half_m, half_m)
 
+
         rest_sb = pool.tile([P, V], F32, name="rest_sb")
-        nc.scalar.activation(out=rest_sb[:], in_=frac_sb[:], func=IDENTITY, bias=one[:], scale=-1.0)
+        nc.scalar.activation(out=rest_sb[:], in_=frac_sb[:], func=COPY, bias=1.0, scale=-1.0)
 
         y = [pool.tile([P, S], F32, name=f"y{t}") for t in range(PACK)]
 
@@ -147,8 +154,8 @@ def tile_picked_lerp_none_lo_kernel(
             nc.scalar.copy(out=y[t][:], in_=acc[:])
 
         last = PACK - 1
-        left_part = pool.tile([P, last, V], F32, name="left_part")
-        right_part = pool.tile([P, last, V], F32, name="right_part")
+        left_part = pool.tile([P, 2, V], F32, name="left_part")
+        right_part = pool.tile([P, 2, V], F32, name="right_part")
         left_last = [pool.tile([P, HALF_V], F32, name=f"left_last{h}") for h in range(2)]
         right_last = [pool.tile([P, HALF_V], F32, name=f"right_last{h}") for h in range(2)]
         result = [pool.tile([P, PACK, HALF_V], F32, name=f"result{h}") for h in range(2)]
@@ -157,12 +164,32 @@ def tile_picked_lerp_none_lo_kernel(
         o_scales = pool.tile([P, V], U8, name="o_scales", align_bytes=64)
         out_rows = out_0.rearrange("(p t) v -> p t v", t=PACK)
 
-        for t in range(last):
-            nc.vector.tensor_tensor(left_part[:, t, :], y[t][:].indirect(left_sb[:]), rest_sb[:], MULT)
-            nc.vector.tensor_tensor(right_part[:, t, :], y[t][:].indirect(right_sb[:]), frac_sb[:], MULT)
-
         def v_cols(h):
             return slice(h * HALF_V, (h + 1) * HALF_V)
+
+        scaled = []
+        for name, places, factor, bank in (("right", right_sb, frac_col, "acc2"), ("left", left_sb, rest_col, "acc3")):
+            found = pool.tile([P, V], F32, name=f"{name}_found")
+            nc.vector.tensor_copy(out=found[:], in_=y[0][:].indirect(places[:]))
+            turned = psum.tile([P, 2, P], F32, name=f"{name}_turned", tag=bank)
+            for h in range(2):
+                nc.tensor.transpose(turned[:, h, :], found[:, v_cols(h)], identity[:])
+            weighted = pool.tile([P, 2, P], F32, name=f"{name}_weighted")
+            for h in range(2):
+                nc.scalar.activation(out=weighted[:, h, :], in_=turned[:, h, :], func=COPY, scale=factor[:, h : h + 1])
+            scaled.append(weighted)
+        summed = psum.tile([P, V], F32, name="summed", tag="first0")
+        for h in range(2):
+            for i in range(2):
+                nc.tensor.matmul(
+                    summed[:, v_cols(h)], scaled[i][:, h, :], identity[:], start=(i == 0), stop=(i == 1), is_transpose=True
+                )
+        for h in range(2):
+            nc.scalar.copy(out=result[h][:, 0, :], in_=summed[:, v_cols(h)])
+
+        for t in range(1, last):
+            nc.vector.tensor_tensor(left_part[:, t - 1, :], y[t][:].indirect(left_sb[:]), rest_sb[:], MULT)
+            nc.vector.tensor_tensor(right_part[:, t - 1, :], y[t][:].indirect(right_sb[:]), frac_sb[:], MULT)
 
         def gather_last(dst, places, factor, h):
             cols = HALF_V // 16
@@ -171,7 +198,7 @@ def tile_picked_lerp_none_lo_kernel(
             )
 
         def add_early(h):
-            nc.vector.tensor_tensor(result[h][:, :last, :], left_part[:, :, v_cols(h)], right_part[:, :, v_cols(h)], ADD)
+            nc.vector.tensor_tensor(result[h][:, 1:last, :], left_part[:, :, v_cols(h)], right_part[:, :, v_cols(h)], ADD)
             nc.sync.dma_start(out=out_rows[:, :last, v_cols(h)], in_=result[h][:, :last, :])
 
         def add_last(h):
@@ -189,11 +216,11 @@ def tile_picked_lerp_none_lo_kernel(
             )
 
         gather_last(left_last, left_sb, rest_sb, 0)
-        add_early(0)
         gather_last(right_last, right_sb, frac_sb, 0)
-        gather_last(left_last, left_sb, rest_sb, 1)
+        add_early(0)
         add_last(0)
         nc.scalar.copy(*round_views(0))
+        gather_last(left_last, left_sb, rest_sb, 1)
         gather_last(right_last, right_sb, frac_sb, 1)
         add_early(1)
         add_last(1)

@@ -143,22 +143,20 @@ def tile_picked_lerp_none_lo_kernel(
                 stop=True,
             )
 
-        first = [psum.tile([P, HALF_S], F32, name=f"first{h}") for h in range(2)]
-        for h in range(2):
-            product(0, first[h][:], slice(h * HALF_S, (h + 1) * HALF_S))
-        for h in range(2):
-            nc.scalar.copy(out=y[0][:, h * HALF_S : (h + 1) * HALF_S], in_=first[h][:])
+        first = [psum.tile([P, P], F32, name=f"first{i}") for i in range(PACK)]
+        for i in range(PACK):
+            product(0, first[i][:], slice(i * P, (i + 1) * P))
+        for i in range(PACK):
+            nc.scalar.copy(out=y[0][:, i * P : (i + 1) * P], in_=first[i][:])
         for t in range(1, PACK):
             acc = psum.tile([P, S], F32, name=f"acc{t}")
             product(t, acc[:], slice(0, S))
             nc.scalar.copy(out=y[t][:], in_=acc[:])
 
         last = PACK - 1
-        left_part = pool.tile([P, 2, V], F32, name="left_part")
-        right_part = pool.tile([P, 2, V], F32, name="right_part")
-        left_last = [pool.tile([P, HALF_V], F32, name=f"left_last{h}") for h in range(2)]
-        right_last = [pool.tile([P, HALF_V], F32, name=f"right_last{h}") for h in range(2)]
-        result = [pool.tile([P, PACK, HALF_V], F32, name=f"result{h}") for h in range(2)]
+        left_part = pool.tile([P, last, V], F32, name="left_part")
+        right_part = pool.tile([P, last, V], F32, name="right_part")
+        result = pool.tile([P, 2, PACK, HALF_V], F32, name="result")
         rounded = [pool.tile([P, HALF_V, PACK], BF16, name=f"rounded{h}", align_bytes=64) for h in range(2)]
         o_codes = pool.tile([P, V], U32, name="o_codes", align_bytes=64)
         o_scales = pool.tile([P, V], U8, name="o_scales", align_bytes=64)
@@ -184,8 +182,8 @@ def tile_picked_lerp_none_lo_kernel(
                 nc.tensor.matmul(
                     summed[:, v_cols(h)], scaled[i][:, h, :], identity[:], start=(i == 0), stop=(i == 1), is_transpose=True
                 )
-        for h in range(2):
-            nc.scalar.copy(out=result[h][:, 0, :], in_=summed[:, v_cols(h)])
+        nc.scalar.copy(out=result[:, :, 0, :], in_=summed[:].rearrange("p (h v) -> p h v", h=2))
+        nc.scalar.dma_start(out=out_rows[:, 0, :].rearrange("p (h v) -> p h v", h=2), in_=result[:, :, 0, :])
 
         for t in range(1, last):
             nc.vector.tensor_tensor(left_part[:, t - 1, :], y[t][:].indirect(left_sb[:]), rest_sb[:], MULT)
@@ -194,19 +192,15 @@ def tile_picked_lerp_none_lo_kernel(
         def gather_last(dst, places, factor, h):
             cols = HALF_V // 16
             nc.vector.tensor_tensor(
-                dst[h][:], y[last][:].indirect(places[:, h * cols : (h + 1) * cols]), factor[:, v_cols(h)], MULT
+                dst[:, last - 1, v_cols(h)], y[last][:].indirect(places[:, h * cols : (h + 1) * cols]), factor[:, v_cols(h)], MULT
             )
 
-        def add_early(h):
-            nc.vector.tensor_tensor(result[h][:, 1:last, :], left_part[:, :, v_cols(h)], right_part[:, :, v_cols(h)], ADD)
-            nc.sync.dma_start(out=out_rows[:, :last, v_cols(h)], in_=result[h][:, :last, :])
-
-        def add_last(h):
-            nc.vector.tensor_tensor(result[h][:, last, :], left_last[h][:], right_last[h][:], ADD)
-            nc.sync.dma_start(out=out_rows[:, last, v_cols(h)], in_=result[h][:, last, :])
+        def add_parts(h):
+            nc.vector.tensor_tensor(result[:, h, 1:, :], left_part[:, :, v_cols(h)], right_part[:, :, v_cols(h)], ADD)
+            nc.sync.dma_start(out=out_rows[:, 1:, v_cols(h)], in_=result[:, h, 1:, :])
 
         def round_views(h):
-            return rounded[h][:], result[h][:].rearrange("p t v -> p v t")
+            return rounded[h][:], result[:, h, :, :].rearrange("p t v -> p v t")
 
         def quantize_result(h):
             nc.vector.quantize_mx(
@@ -215,17 +209,14 @@ def tile_picked_lerp_none_lo_kernel(
                 in_=rounded[h][:].rearrange("p v t -> p (v t)"),
             )
 
-        gather_last(left_last, left_sb, rest_sb, 0)
-        gather_last(right_last, right_sb, frac_sb, 0)
-        add_early(0)
-        add_last(0)
+        nc.vector.tensor_tensor(left_part[:, last - 1, :], y[last][:].indirect(left_sb[:]), rest_sb[:], MULT)
+        gather_last(right_part, right_sb, frac_sb, 0)
+        gather_last(right_part, right_sb, frac_sb, 1)
+        add_parts(0)
         nc.scalar.copy(*round_views(0))
-        gather_last(left_last, left_sb, rest_sb, 1)
-        gather_last(right_last, right_sb, frac_sb, 1)
-        add_early(1)
-        add_last(1)
-        quantize_result(0)
+        add_parts(1)
         nc.vector.tensor_copy(*round_views(1))
+        quantize_result(0)
         quantize_result(1)
 
         nc.sync.dma_start(

@@ -55,10 +55,8 @@ def tile_picked_lerp_none_lo_kernel(
         nc.sync.dma_start(left_sb[:], left)
 
         frac_col = pool.tile([P, 2], F32, name="frac_col")
-        rest_col = pool.tile([P, 2], F32, name="rest_col")
         with nc.allow_non_contiguous_dma(reason="one value of frac a partition"):
             nc.sync.dma_start(out=frac_col[:], in_=frac[0, :].rearrange("(h p) -> p h", p=P))
-        nc.scalar.activation(out=rest_col[:], in_=frac_col[:], func=COPY, bias=1.0, scale=-1.0)
 
         identity = pool.tile([P, P], F32, name="identity")
         make_identity(nc, identity[:])
@@ -110,7 +108,7 @@ def tile_picked_lerp_none_lo_kernel(
             )
 
         w_front = reused.tile([P, 2, P, PACK], BF16, name="w_front", align_bytes=64, offset=0)
-        w_back1 = pool.tile([P, 2, half_m, PACK], BF16, name="w_back1", align_bytes=64)
+        w_back1 = reused.tile([P, 2, half_m, PACK], BF16, name="w_back1", align_bytes=64, offset=P * PACK * 4)
         for h in range(2):
             dst = w_front[:, :, h * half_m : (h + 1) * half_m, :]
             nc.scalar.copy(out=dst.rearrange("p t m j -> p m j t"), in_=deal_source(0, h))
@@ -126,8 +124,11 @@ def tile_picked_lerp_none_lo_kernel(
                 quantize_w(back[:, t - 2, :, :], t * P + h * half_m, half_m)
 
 
-        rest_sb = pool.tile([P, V], F32, name="rest_sb")
-        nc.scalar.activation(out=rest_sb[:], in_=frac_sb[:], func=COPY, bias=1.0, scale=-1.0)
+        rest_sb = reused.tile([P, V], F32, name="rest_sb", align_bytes=64, offset=P * PACK * 2)
+        nc.vector.tensor_scalar(rest_sb[:], frac_sb[:], -1.0, 1.0, MULT, ADD)
+
+        rest_col = reused.tile([P, 2], F32, name="rest_col", align_bytes=64, offset=P * PACK * 4)
+        nc.scalar.activation(out=rest_col[:], in_=frac_col[:], func=COPY, bias=1.0, scale=-1.0)
 
         y = [pool.tile([P, S], F32, name=f"y{t}") for t in range(PACK)]
 
@@ -189,6 +190,17 @@ def tile_picked_lerp_none_lo_kernel(
             nc.vector.tensor_tensor(left_part[:, t - 1, :], y[t][:].indirect(left_sb[:]), rest_sb[:], MULT)
             nc.vector.tensor_tensor(right_part[:, t - 1, :], y[t][:].indirect(right_sb[:]), frac_sb[:], MULT)
 
+        second_turned = psum.tile([P, P], F32, name="second_turned", tag="acc3")
+        for i, part in enumerate((left_part, right_part)):
+            nc.tensor.matmul(
+                second_turned[:], part[:, 0, v_cols(1)], identity[:], start=(i == 0), stop=(i == 1), is_transpose=True
+            )
+        second_sum = pool.tile([P, P], F32, name="second_sum")
+        nc.scalar.copy(out=second_sum[:], in_=second_turned[:])
+        second_back = psum.tile([P, P], F32, name="second_back", tag="acc2")
+        nc.tensor.transpose(second_back[:], second_sum[:], identity[:])
+        nc.scalar.copy(out=result[:, 1, 1, :], in_=second_back[:])
+
         def gather_last(dst, places, factor, h):
             cols = HALF_V // 16
             nc.vector.tensor_tensor(
@@ -196,7 +208,9 @@ def tile_picked_lerp_none_lo_kernel(
             )
 
         def add_parts(h):
-            nc.vector.tensor_tensor(result[:, h, 1:, :], left_part[:, :, v_cols(h)], right_part[:, :, v_cols(h)], ADD)
+            nc.vector.tensor_tensor(
+                result[:, h, 1 + h :, :], left_part[:, h:, v_cols(h)], right_part[:, h:, v_cols(h)], ADD
+            )
             nc.sync.dma_start(out=out_rows[:, 1:, v_cols(h)], in_=result[:, h, 1:, :])
 
         def round_views(h):

@@ -155,9 +155,9 @@ def tile_picked_lerp_none_lo_kernel(
             nc.scalar.copy(out=y[t][:], in_=acc[:])
 
         last = PACK - 1
-        left_part = pool.tile([P, last, V], F32, name="left_part")
-        right_part = pool.tile([P, last, V], F32, name="right_part")
-        result = pool.tile([P, 2, PACK, HALF_V], F32, name="result")
+        left_part = pool.tile([P, 2, V], F32, name="left_part")
+        right_part = pool.tile([P, 2, V], F32, name="right_part")
+        result = pool.tile([P, PACK, V], F32, name="result")
         rounded = [pool.tile([P, HALF_V, PACK], BF16, name=f"rounded{h}", align_bytes=64) for h in range(2)]
         o_codes = pool.tile([P, V], U32, name="o_codes", align_bytes=64)
         o_scales = pool.tile([P, V], U8, name="o_scales", align_bytes=64)
@@ -166,55 +166,47 @@ def tile_picked_lerp_none_lo_kernel(
         def v_cols(h):
             return slice(h * HALF_V, (h + 1) * HALF_V)
 
-        scaled = []
-        for name, places, factor, bank in (("right", right_sb, frac_col, "acc2"), ("left", left_sb, rest_col, "acc3")):
-            found = pool.tile([P, V], F32, name=f"{name}_found")
-            nc.vector.tensor_copy(out=found[:], in_=y[0][:].indirect(places[:]))
-            turned = psum.tile([P, 2, P], F32, name=f"{name}_turned", tag=bank)
+        def mix_turned(t, banks):
+            scaled = []
+            for name, places, factor, bank in (("right", right_sb, frac_col, banks[0]), ("left", left_sb, rest_col, banks[1])):
+                found = pool.tile([P, V], F32, name=f"{name}_found{t}")
+                nc.vector.tensor_copy(out=found[:], in_=y[t][:].indirect(places[:]))
+                turned = psum.tile([P, 2, P], F32, name=f"{name}_turned{t}", tag=bank)
+                for h in range(2):
+                    nc.tensor.transpose(turned[:, h, :], found[:, v_cols(h)], identity[:])
+                weighted = pool.tile([P, 2, P], F32, name=f"{name}_weighted{t}")
+                for h in range(2):
+                    nc.scalar.activation(out=weighted[:, h, :], in_=turned[:, h, :], func=COPY, scale=factor[:, h : h + 1])
+                scaled.append(weighted)
+            summed = psum.tile([P, V], F32, name=f"summed{t}", tag=banks[2])
             for h in range(2):
-                nc.tensor.transpose(turned[:, h, :], found[:, v_cols(h)], identity[:])
-            weighted = pool.tile([P, 2, P], F32, name=f"{name}_weighted")
-            for h in range(2):
-                nc.scalar.activation(out=weighted[:, h, :], in_=turned[:, h, :], func=COPY, scale=factor[:, h : h + 1])
-            scaled.append(weighted)
-        summed = psum.tile([P, V], F32, name="summed", tag="first0")
-        for h in range(2):
-            for i in range(2):
-                nc.tensor.matmul(
-                    summed[:, v_cols(h)], scaled[i][:, h, :], identity[:], start=(i == 0), stop=(i == 1), is_transpose=True
-                )
-        nc.scalar.copy(out=result[:, :, 0, :], in_=summed[:].rearrange("p (h v) -> p h v", h=2))
-        nc.scalar.dma_start(out=out_rows[:, 0, :].rearrange("p (h v) -> p h v", h=2), in_=result[:, :, 0, :])
+                for i in range(2):
+                    nc.tensor.matmul(
+                        summed[:, v_cols(h)], scaled[i][:, h, :], identity[:], start=(i == 0), stop=(i == 1), is_transpose=True
+                    )
+            nc.scalar.copy(out=result[:, t, :], in_=summed[:])
 
-        for t in range(1, last):
-            nc.vector.tensor_tensor(left_part[:, t - 1, :], y[t][:].indirect(left_sb[:]), rest_sb[:], MULT)
-            nc.vector.tensor_tensor(right_part[:, t - 1, :], y[t][:].indirect(right_sb[:]), frac_sb[:], MULT)
+        mix_turned(0, ("first0", "first1", "spare"))
+        mix_turned(1, ("first2", "first3", "acc1"))
+        nc.scalar.dma_start(out=out_rows[:, 0:2, :], in_=result[:, 0:2, :])
 
-        second_turned = psum.tile([P, P], F32, name="second_turned", tag="acc3")
-        for i, part in enumerate((left_part, right_part)):
-            nc.tensor.matmul(
-                second_turned[:], part[:, 0, v_cols(1)], identity[:], start=(i == 0), stop=(i == 1), is_transpose=True
-            )
-        second_sum = pool.tile([P, P], F32, name="second_sum")
-        nc.scalar.copy(out=second_sum[:], in_=second_turned[:])
-        second_back = psum.tile([P, P], F32, name="second_back", tag="acc2")
-        nc.tensor.transpose(second_back[:], second_sum[:], identity[:])
-        nc.scalar.copy(out=result[:, 1, 1, :], in_=second_back[:])
+        nc.vector.tensor_tensor(left_part[:, 0, :], y[2][:].indirect(left_sb[:]), rest_sb[:], MULT)
+        nc.vector.tensor_tensor(right_part[:, 0, :], y[2][:].indirect(right_sb[:]), frac_sb[:], MULT)
 
         def gather_last(dst, places, factor, h):
             cols = HALF_V // 16
             nc.vector.tensor_tensor(
-                dst[:, last - 1, v_cols(h)], y[last][:].indirect(places[:, h * cols : (h + 1) * cols]), factor[:, v_cols(h)], MULT
+                dst[:, 1, v_cols(h)], y[last][:].indirect(places[:, h * cols : (h + 1) * cols]), factor[:, v_cols(h)], MULT
             )
 
         def add_parts(h):
             nc.vector.tensor_tensor(
-                result[:, h, 1 + h :, :], left_part[:, h:, v_cols(h)], right_part[:, h:, v_cols(h)], ADD
+                result[:, 2:, v_cols(h)], left_part[:, :, v_cols(h)], right_part[:, :, v_cols(h)], ADD
             )
-            nc.sync.dma_start(out=out_rows[:, 1:, v_cols(h)], in_=result[:, h, 1:, :])
+            nc.sync.dma_start(out=out_rows[:, 2:, v_cols(h)], in_=result[:, 2:, v_cols(h)])
 
         def round_views(h):
-            return rounded[h][:], result[:, h, :, :].rearrange("p t v -> p v t")
+            return rounded[h][:], result[:, :, v_cols(h)].rearrange("p t v -> p v t")
 
         def quantize_result(h):
             nc.vector.quantize_mx(
@@ -223,7 +215,7 @@ def tile_picked_lerp_none_lo_kernel(
                 in_=rounded[h][:].rearrange("p v t -> p (v t)"),
             )
 
-        nc.vector.tensor_tensor(left_part[:, last - 1, :], y[last][:].indirect(left_sb[:]), rest_sb[:], MULT)
+        nc.vector.tensor_tensor(left_part[:, 1, :], y[last][:].indirect(left_sb[:]), rest_sb[:], MULT)
         gather_last(right_part, right_sb, frac_sb, 0)
         gather_last(right_part, right_sb, frac_sb, 1)
         add_parts(0)

@@ -22,6 +22,7 @@ PACK = 4
 HALF_S = S // 2
 HALF_N = N // 2
 HALF_V = V // 2
+SCALAR_ROUNDS = 64
 
 
 def tile_picked_lerp_none_lo_kernel(
@@ -158,7 +159,8 @@ def tile_picked_lerp_none_lo_kernel(
         left_part = pool.tile([P, 2, V], F32, name="left_part")
         right_part = pool.tile([P, 2, V], F32, name="right_part")
         result = pool.tile([P, PACK, V], F32, name="result")
-        rounded = [pool.tile([P, HALF_V, PACK], BF16, name=f"rounded{h}", align_bytes=64) for h in range(2)]
+        pieces = ((0, SCALAR_ROUNDS), (SCALAR_ROUNDS, HALF_V), (HALF_V, V))
+        rounded = [pool.tile([P, v1 - v0, PACK], BF16, name=f"rounded{v0}", align_bytes=64) for v0, v1 in pieces]
         o_codes = pool.tile([P, V], U32, name="o_codes", align_bytes=64)
         o_scales = pool.tile([P, V], U8, name="o_scales", align_bytes=64)
         out_rows = out_0.rearrange("(p t) v -> p t v", t=PACK)
@@ -205,14 +207,14 @@ def tile_picked_lerp_none_lo_kernel(
             )
             nc.sync.dma_start(out=out_rows[:, 2:, v_cols(h)], in_=result[:, 2:, v_cols(h)])
 
-        def round_views(h):
-            return rounded[h][:], result[:, :, v_cols(h)].rearrange("p t v -> p v t")
+        def round_views(i):
+            return rounded[i][:], result[:, :, slice(*pieces[i])].rearrange("p t v -> p v t")
 
-        def quantize_result(h):
+        def quantize_result(i):
             nc.vector.quantize_mx(
-                out=o_codes[:, v_cols(h)].bitcast(FP8X4),
-                scales=o_scales[:, v_cols(h)],
-                in_=rounded[h][:].rearrange("p v t -> p (v t)"),
+                out=o_codes[:, slice(*pieces[i])].bitcast(FP8X4),
+                scales=o_scales[:, slice(*pieces[i])],
+                in_=rounded[i][:].rearrange("p v t -> p (v t)"),
             )
 
         nc.vector.tensor_tensor(left_part[:, 1, :], y[last][:].indirect(left_sb[:]), rest_sb[:], MULT)
@@ -222,8 +224,9 @@ def tile_picked_lerp_none_lo_kernel(
         nc.scalar.copy(*round_views(0))
         add_parts(1)
         nc.vector.tensor_copy(*round_views(1))
-        quantize_result(0)
-        quantize_result(1)
+        nc.vector.tensor_copy(*round_views(2))
+        for i in (1, 0, 2):
+            quantize_result(i)
 
         nc.sync.dma_start(
             out=out_1.rearrange("z p c r -> p (z c r)").bitcast(I32), in_=o_codes[:].bitcast(I32)

@@ -42,7 +42,7 @@ def tile_picked_lerp_none_lo_kernel(
         x_rows = xT.rearrange("(p j) t -> p j t", j=PACK)
         w_rows = w1.rearrange("(p j) m -> p j m", j=PACK)
         x_raw = [pool.tile([P, T], F32, name=f"x_raw{j}") for j in range(PACK)]
-        w_raw = [pool.tile([P, PACK, HALF_N], F32, name=f"w_raw{h}") for h in range(2)]
+        w_raw = [reused.tile([P, PACK, HALF_N], F32, name=f"w_raw{h}", offset=8192 + h * 4096) for h in range(2)]
         frac_sb = pool.tile([P, V], F32, name="frac_sb")
 
         nc.sync.dma_start(out=x_raw[0][:], in_=x_rows[:, 0, :])
@@ -51,10 +51,9 @@ def tile_picked_lerp_none_lo_kernel(
             nc.sync.dma_start(out=x_raw[j][:], in_=x_rows[:, j, :])
         for h in range(2):
             nc.sync.dma_start(out=w_raw[h][:], in_=w_rows[:, :, h * HALF_N : (h + 1) * HALF_N])
-        nc.sync.dma_start(out=frac_sb[:], in_=frac)
         nc.sync.dma_start(right_sb[:], right)
         nc.sync.dma_start(left_sb[:], left)
-
+        nc.sync.dma_start(out=frac_sb[:], in_=frac)
         frac_col = pool.tile([P, 2], F32, name="frac_col")
         with nc.allow_non_contiguous_dma(reason="one value of frac a partition"):
             nc.sync.dma_start(out=frac_col[:], in_=frac[0, :].rearrange("(h p) -> p h", p=P))
@@ -63,9 +62,10 @@ def tile_picked_lerp_none_lo_kernel(
         make_identity(nc, identity[:])
 
         x_found = [pool.tile([P, 2, S], F32, name=f"x_found{u}") for u in range(2)]
-        x_picked = [pool.tile([P, HALF_S, PACK], BF16, name=f"x_picked{h}", align_bytes=64) for h in range(2)]
+        x_picked = [
+            reused.tile([P, HALF_S, PACK], BF16, name=f"x_picked{h}", align_bytes=64, offset=4096 + h * 2048) for h in range(2)
+        ]
         x_codes = pool.tile([P, S], U32, name="x_codes", align_bytes=64)
-        x_scales = pool.tile([P, S], U8, name="x_scales", align_bytes=64)
 
         def weave_views(u, h):
             dst = x_picked[h][:, :, 2 * u : 2 * u + 2]
@@ -95,41 +95,40 @@ def tile_picked_lerp_none_lo_kernel(
             )
 
         w_codes = pool.tile([P, N], U32, name="w_codes", align_bytes=64)
-        w_scales = pool.tile([P, N], U8, name="w_scales", align_bytes=64)
+        front_scales = pool.tile([P, HALF_N], U8, name="front_scales", align_bytes=64)
         half_m = P // 2
 
         def deal_source(u, h):
             return w_raw[h][:].rearrange("p j (m t) -> p m j t", t=PACK)[:, :, :, 2 * u : 2 * u + 2]
 
-        def quantize_w(src, c0, width):
+        def quantize_w(src, c0, width, scales):
             nc.vector.quantize_mx(
                 out=w_codes[:, c0 : c0 + width].bitcast(FP8X4),
-                scales=w_scales[:, c0 : c0 + width],
-                in_=src.rearrange("p m j -> p (m j)"),
+                scales=scales,
+                in_=src,
             )
 
-        w_front = reused.tile([P, 2, P, PACK], BF16, name="w_front", align_bytes=64, offset=0)
-        w_back1 = reused.tile([P, 2, half_m, PACK], BF16, name="w_back1", align_bytes=64, offset=P * PACK * 4)
-        for h in range(2):
-            dst = w_front[:, :, h * half_m : (h + 1) * half_m, :]
-            nc.scalar.copy(out=dst.rearrange("p t m j -> p m j t"), in_=deal_source(0, h))
-        nc.scalar.copy(out=w_back1[:].rearrange("p t m j -> p m j t"), in_=deal_source(1, 1))
+        w_front = [
+            reused.tile([P, P * PACK], BF16, name=f"w_front{h}", align_bytes=64, offset=h * P * PACK * 2) for h in range(2)
+        ]
+        w_back = pool.tile([P, 2 * P * PACK], BF16, name="w_back", align_bytes=64)
+
+        def dealt(dst):
+            return dst.rearrange("p (t m j) -> p m j t", t=2, j=PACK)
+
+        nc.scalar.copy(out=dealt(w_front[0][:]), in_=deal_source(0, 0))
+        nc.scalar.copy(out=dealt(w_back[:])[:, 0:half_m, :, :], in_=deal_source(1, 0))
+        nc.scalar.copy(out=dealt(w_front[1][:]), in_=deal_source(0, 1))
+        quantize_w(w_front[0][:], 0, P, front_scales[:, 0:P])
+        x_scales = reused.tile([P, S], U8, name="x_scales", align_bytes=64, offset=0)
         quantize_x(0)
-        quantize_w(w_front[:, 0, :, :], 0, P)
         quantize_x(1)
-        quantize_w(w_front[:, 1, :, :], P, P)
-        w_back0 = reused.tile([P, 2, half_m, PACK], BF16, name="w_back0", align_bytes=64, offset=0)
-        nc.vector.tensor_copy(out=w_back0[:].rearrange("p t m j -> p m j t"), in_=deal_source(1, 0))
-        for h, back in ((1, w_back1), (0, w_back0)):
-            for t in (2, 3):
-                quantize_w(back[:, t - 2, :, :], t * P + h * half_m, half_m)
-
-
-        rest_sb = reused.tile([P, V], F32, name="rest_sb", align_bytes=64, offset=P * PACK * 2)
+        nc.vector.tensor_copy(out=dealt(w_back[:])[:, half_m:, :, :], in_=deal_source(1, 1))
+        quantize_w(w_front[1][:], P, P, front_scales[:, P:])
+        back_scales = reused.tile([P, HALF_N], U8, name="back_scales", align_bytes=64, offset=8192 + 4096)
+        quantize_w(w_back[:], 2 * P, 2 * P, back_scales[:])
+        rest_sb = reused.tile([P, V], F32, name="rest_sb", align_bytes=64, offset=4096 + 2048)
         nc.vector.tensor_scalar(rest_sb[:], frac_sb[:], -1.0, 1.0, MULT, ADD)
-
-        rest_col = reused.tile([P, 2], F32, name="rest_col", align_bytes=64, offset=P * PACK * 4)
-        nc.scalar.activation(out=rest_col[:], in_=frac_col[:], func=COPY, bias=1.0, scale=-1.0)
 
         y = [pool.tile([P, S], F32, name=f"y{t}") for t in range(PACK)]
 
@@ -138,7 +137,7 @@ def tile_picked_lerp_none_lo_kernel(
             nc.tensor.matmul_mx(
                 out=acc,
                 lhsT=w_codes[:, rows].bitcast(FP8X4),
-                lhsT_scale=w_scales[:, rows],
+                lhsT_scale=(front_scales, back_scales)[t // 2][:, (t % 2) * P : (t % 2 + 1) * P],
                 rhs=x_codes[:, cols].bitcast(FP8X4),
                 rhs_scale=x_scales[:, cols],
                 start=True,
@@ -155,6 +154,9 @@ def tile_picked_lerp_none_lo_kernel(
             product(t, acc[:], slice(0, S))
             nc.scalar.copy(out=y[t][:], in_=acc[:])
 
+        rest_col = pool.tile([P, 2], F32, name="rest_col")
+        nc.scalar.activation(out=rest_col[:], in_=frac_col[:], func=COPY, bias=1.0, scale=-1.0)
+
         last = PACK - 1
         left_part = pool.tile([P, 2, V], F32, name="left_part")
         right_part = pool.tile([P, 2, V], F32, name="right_part")
@@ -168,28 +170,39 @@ def tile_picked_lerp_none_lo_kernel(
         def v_cols(h):
             return slice(h * HALF_V, (h + 1) * HALF_V)
 
-        def mix_turned(t, banks):
-            scaled = []
-            for name, places, factor, bank in (("right", right_sb, frac_col, banks[0]), ("left", left_sb, rest_col, banks[1])):
-                found = pool.tile([P, V], F32, name=f"{name}_found{t}")
-                nc.vector.tensor_copy(out=found[:], in_=y[t][:].indirect(places[:]))
-                turned = psum.tile([P, 2, P], F32, name=f"{name}_turned{t}", tag=bank)
+        weighted = [pool.tile([P, 2, 2, P], F32, name=f"weighted{i}") for i in range(2)]
+
+        founds = [pool.tile([P, V], F32, name=f"found{n}") for n in range(4)]
+
+        def weigh_turned(a, banks):
+            for i, (places, factor) in enumerate(((right_sb, frac_col), (left_sb, rest_col))):
+                found = founds[2 * a + i]
+                nc.vector.tensor_copy(out=found[:], in_=y[a][:].indirect(places[:]))
+                turned = psum.tile([P, 2, P], F32, name=f"turned{i}{a}", tag=banks[i])
                 for h in range(2):
                     nc.tensor.transpose(turned[:, h, :], found[:, v_cols(h)], identity[:])
-                weighted = pool.tile([P, 2, P], F32, name=f"{name}_weighted{t}")
                 for h in range(2):
-                    nc.scalar.activation(out=weighted[:, h, :], in_=turned[:, h, :], func=COPY, scale=factor[:, h : h + 1])
-                scaled.append(weighted)
-            summed = psum.tile([P, V], F32, name=f"summed{t}", tag=banks[2])
-            for h in range(2):
-                for i in range(2):
-                    nc.tensor.matmul(
-                        summed[:, v_cols(h)], scaled[i][:, h, :], identity[:], start=(i == 0), stop=(i == 1), is_transpose=True
+                    nc.scalar.activation(
+                        out=weighted[i][:, h, :, a * half_m : (a + 1) * half_m],
+                        in_=turned[:, h, :].rearrange("p (t m) -> p t m", t=2),
+                        func=COPY,
+                        scale=factor[:, h : h + 1],
                     )
-            nc.scalar.copy(out=result[:, t, :], in_=summed[:])
 
-        mix_turned(0, ("first0", "first1", "spare"))
-        mix_turned(1, ("first2", "first3", "acc1"))
+        weigh_turned(0, ("first0", "first1"))
+        weigh_turned(1, ("first2", "first3"))
+        summed = psum.tile([P, 2, V], F32, name="summed")
+        turns = [(i, h, t) for i in range(2) for h in range(2) for t in range(2)]
+        for i, h, t in turns:
+            nc.tensor.matmul(
+                summed[:, t, v_cols(h)],
+                weighted[i][:, h, t, :],
+                identity[:],
+                start=(i, h, t) == turns[0],
+                stop=(i, h, t) == turns[-1],
+                is_transpose=True,
+            )
+        nc.scalar.copy(out=result[:, 0:2, :], in_=summed[:])
         nc.scalar.dma_start(out=out_rows[:, 0:2, :], in_=result[:, 0:2, :])
 
         nc.vector.tensor_tensor(left_part[:, 0, :], y[2][:].indirect(left_sb[:]), rest_sb[:], MULT)

@@ -86,12 +86,12 @@ def tile_picked_lerp_none_lo_kernel(
         for h in range(2):
             nc.vector.tensor_copy(*weave_views(1, h))
 
-        def quantize_x(h):
-            cols = slice(h * HALF_S, (h + 1) * HALF_S)
+        def quantize_x(h, c0, c1):
+            cols = slice(h * HALF_S + c0, h * HALF_S + c1)
             nc.vector.quantize_mx(
                 out=x_codes[:, cols].bitcast(FP8X4),
                 scales=x_scales[:, cols],
-                in_=x_picked[h][:].rearrange("p s j -> p (s j)"),
+                in_=x_picked[h][:, c0:c1, :].rearrange("p s j -> p (s j)"),
             )
 
         w_codes = pool.tile([P, N], U32, name="w_codes", align_bytes=64)
@@ -121,8 +121,9 @@ def tile_picked_lerp_none_lo_kernel(
         nc.scalar.copy(out=dealt(w_front[1][:]), in_=deal_source(0, 1))
         quantize_w(w_front[0][:], 0, P, front_scales[:, 0:P])
         x_scales = reused.tile([P, S], U8, name="x_scales", align_bytes=64, offset=0)
-        quantize_x(0)
-        quantize_x(1)
+        quantize_x(0, 0, HALF_S)
+        quantize_x(1, 0, P)
+        quantize_x(1, P, HALF_S)
         nc.vector.tensor_copy(out=dealt(w_back[:])[:, half_m:, :, :], in_=deal_source(1, 1))
         quantize_w(w_front[1][:], P, P, front_scales[:, P:])
         back_scales = reused.tile([P, HALF_N], U8, name="back_scales", align_bytes=64, offset=8192 + 4096)
@@ -221,7 +222,8 @@ def tile_picked_lerp_none_lo_kernel(
             nc.sync.dma_start(out=out_rows[:, 2:, v_cols(h)], in_=result[:, 2:, v_cols(h)])
 
         def round_views(i):
-            return rounded[i][:], result[:, :, slice(*pieces[i])].rearrange("p t v -> p v t")
+            dst = rounded[i][:].rearrange("p (c n) t -> p c t n", n=PACK)
+            return dst, result[:, :, slice(*pieces[i])].rearrange("p t (c n) -> p c t n", n=PACK)
 
         def quantize_result(i):
             nc.vector.quantize_mx(

@@ -150,10 +150,11 @@ def tile_picked_lerp_none_lo_kernel(
             product(0, first[i][:], slice(i * P, (i + 1) * P))
         for i in range(PACK):
             nc.scalar.copy(out=y[0][:, i * P : (i + 1) * P], in_=first[i][:])
-        for t in range(1, PACK):
-            acc = psum.tile([P, S], F32, name=f"acc{t}")
-            product(t, acc[:], slice(0, S))
-            nc.scalar.copy(out=y[t][:], in_=acc[:])
+        acc = {t: psum.tile([P, S], F32, name=f"acc{t}") for t in (1, 3, 2)}
+        for t in acc:
+            product(t, acc[t][:], slice(0, S))
+        for t, cols in ((1, slice(0, S)), (3, slice(0, HALF_S)), (2, slice(0, S)), (3, slice(HALF_S, S))):
+            nc.scalar.copy(out=y[t][:, cols], in_=acc[t][:, cols])
 
         rest_col = pool.tile([P, 2], F32, name="rest_col")
         nc.scalar.activation(out=rest_col[:], in_=frac_col[:], func=COPY, bias=1.0, scale=-1.0)
@@ -217,9 +218,8 @@ def tile_picked_lerp_none_lo_kernel(
 
         def add_parts(h):
             nc.vector.tensor_tensor(
-                result[:, 2:, v_cols(h)], left_part[:, :, v_cols(h)], right_part[:, :, v_cols(h)], ADD
+                result[:, last, v_cols(h)], left_part[:, 1, v_cols(h)], right_part[:, 1, v_cols(h)], ADD
             )
-            nc.sync.dma_start(out=out_rows[:, 2:, v_cols(h)], in_=result[:, 2:, v_cols(h)])
 
         def round_views(i):
             dst = rounded[i][:].rearrange("p (c n) t -> p c t n", n=PACK)
@@ -233,11 +233,14 @@ def tile_picked_lerp_none_lo_kernel(
             )
 
         nc.vector.tensor_tensor(left_part[:, 1, :], y[last][:].indirect(left_sb[:]), rest_sb[:], MULT)
+        nc.vector.tensor_tensor(result[:, 2, :], left_part[:, 0, :], right_part[:, 0, :], ADD)
+        nc.sync.dma_start(out=out_rows[:, 2, :], in_=result[:, 2, :])
         gather_last(right_part, right_sb, frac_sb, 0)
         gather_last(right_part, right_sb, frac_sb, 1)
         add_parts(0)
         nc.scalar.copy(*round_views(0))
         add_parts(1)
+        nc.sync.dma_start(out=out_rows[:, last, :], in_=result[:, last, :])
         nc.vector.tensor_copy(*round_views(1))
         nc.vector.tensor_copy(*round_views(2))
         for i in (1, 0, 2):

@@ -1,7 +1,6 @@
 from contextlib import ExitStack
 
 import concourse.mybir as mybir
-from concourse.masks import make_identity
 
 K, T, S, V, N = 512, 1024, 512, 256, 512
 FLOPS = 2 * K * N * S
@@ -21,6 +20,7 @@ P = 128
 PACK = 4
 HALF_S = S // 2
 HALF_N = N // 2
+HALF_M = P // 2
 HALF_V = V // 2
 SCALAR_ROUNDS = 64
 
@@ -32,7 +32,6 @@ def tile_picked_lerp_none_lo_kernel(
     with ExitStack() as ctx:
         lists = ctx.enter_context(tc.tile_pool(name="lists", bufs=1))
         pool = ctx.enter_context(tc.tile_pool(name="pool", bufs=1))
-        reused = ctx.enter_context(tc.tile_pool(name="reused", bufs=1))
         psum = ctx.enter_context(tc.psum_pool(name="psum", bufs=1))
 
         offs_sb = lists.tile([P, S // 16], U16, name="offs_sb")
@@ -42,7 +41,7 @@ def tile_picked_lerp_none_lo_kernel(
         x_rows = xT.rearrange("(p j) t -> p j t", j=PACK)
         w_rows = w1.rearrange("(p j) m -> p j m", j=PACK)
         x_raw = [pool.tile([P, T], F32, name=f"x_raw{j}") for j in range(PACK)]
-        w_raw = [reused.tile([P, PACK, HALF_N], F32, name=f"w_raw{h}", offset=8192 + h * 4096) for h in range(2)]
+        w_raw = [pool.tile([P, PACK, HALF_N], F32, name=f"w_raw{h}") for h in range(2)]
         frac_sb = pool.tile([P, V], F32, name="frac_sb")
 
         nc.sync.dma_start(out=x_raw[0][:], in_=x_rows[:, 0, :])
@@ -54,93 +53,86 @@ def tile_picked_lerp_none_lo_kernel(
         nc.sync.dma_start(right_sb[:], right)
         nc.sync.dma_start(left_sb[:], left)
         nc.sync.dma_start(out=frac_sb[:], in_=frac)
-        frac_col = pool.tile([P, 2], F32, name="frac_col")
-        with nc.allow_non_contiguous_dma(reason="one value of frac a partition"):
-            nc.sync.dma_start(out=frac_col[:], in_=frac[0, :].rearrange("(h p) -> p h", p=P))
 
-        identity = pool.tile([P, P], F32, name="identity")
-        make_identity(nc, identity[:])
+        idle = pool.tile([P, 2], F32, name="idle")
+        nc.gpsimd.memset(idle[:, 0:1], 0.0)
+        nc.scalar.copy(out=idle[:, 1:2], in_=idle[:, 0:1])
 
-        x_found = [pool.tile([P, 2, S], F32, name=f"x_found{u}") for u in range(2)]
-        x_picked = [
-            reused.tile([P, HALF_S, PACK], BF16, name=f"x_picked{h}", align_bytes=64, offset=4096 + h * 2048) for h in range(2)
-        ]
+        x_found = [[pool.tile([P, 2, HALF_S], F32, name=f"x_found{u}{h}") for h in range(2)] for u in range(2)]
+        x_pieces = ((0, HALF_S), (HALF_S, HALF_S + P), (HALF_S + P, S))
+        x_picked = [pool.tile([P, s1 - s0, PACK], BF16, name=f"x_picked{s0}", align_bytes=64) for s0, s1 in x_pieces]
         x_codes = pool.tile([P, S], U32, name="x_codes", align_bytes=64)
+        x_scales = pool.tile([P, S], U8, name="x_scales", align_bytes=64)
 
-        def weave_views(u, h):
-            dst = x_picked[h][:, :, 2 * u : 2 * u + 2]
-            src = x_found[u][:, :, h * HALF_S : (h + 1) * HALF_S].rearrange("p j s -> p s j")
-            return dst, src
+        def weave_views(u, i):
+            s0, s1 = x_pieces[i]
+            h = s0 // HALF_S
+            src = x_found[u][h][:, :, s0 - h * HALF_S : s1 - h * HALF_S].rearrange("p j s -> p s j")
+            return x_picked[i][:, :, 2 * u : 2 * u + 2], src
 
-        for j in range(PACK - 1):
-            nc.vector.tensor_copy(out=x_found[j // 2][:, j % 2, :], in_=x_raw[j][:].indirect(offs_sb[:]))
+        def pick_views(j, s0, s1):
+            h = s0 // HALF_S
+            dst = x_found[j // 2][h][:, j % 2, s0 - h * HALF_S : s1 - h * HALF_S]
+            return dst, x_raw[j][:].indirect(offs_sb[:, s0 // 16 : s1 // 16])
+
+        for j in range(PACK):
+            border = P if j == 2 else HALF_S
+            nc.vector.tensor_copy(*pick_views(j, 0, border))
+            if border < HALF_S:
+                nc.scalar.activation(*pick_views(j, border, HALF_S), COPY)
+            nc.scalar.activation(*pick_views(j, HALF_S, S), COPY)
             if j == 1:
-                for h in range(2):
-                    nc.scalar.copy(*weave_views(0, h))
-        for h in range(2):
-            cols = HALF_S // 16
-            nc.vector.tensor_copy(
-                out=x_found[1][:, 1, h * HALF_S : (h + 1) * HALF_S],
-                in_=x_raw[PACK - 1][:].indirect(offs_sb[:, h * cols : (h + 1) * cols]),
-            )
-        for h in range(2):
-            nc.vector.tensor_copy(*weave_views(1, h))
-
-        def quantize_x(h, c0, c1):
-            cols = slice(h * HALF_S + c0, h * HALF_S + c1)
+                for i in range(3):
+                    nc.vector.tensor_copy(*weave_views(0, i))
+        nc.vector.tensor_copy(*weave_views(1, 0))
+        nc.scalar.copy(*weave_views(1, 1))
+        nc.vector.tensor_copy(*weave_views(1, 2))
+        for i, (s0, s1) in enumerate(x_pieces):
             nc.vector.quantize_mx(
-                out=x_codes[:, cols].bitcast(FP8X4),
-                scales=x_scales[:, cols],
-                in_=x_picked[h][:, c0:c1, :].rearrange("p s j -> p (s j)"),
+                out=x_codes[:, s0:s1].bitcast(FP8X4),
+                scales=x_scales[:, s0:s1],
+                in_=x_picked[i][:].rearrange("p s j -> p (s j)"),
             )
 
         w_codes = pool.tile([P, N], U32, name="w_codes", align_bytes=64)
-        front_scales = pool.tile([P, HALF_N], U8, name="front_scales", align_bytes=64)
-        half_m = P // 2
+        w_scales = pool.tile([P, N], U8, name="w_scales", align_bytes=64)
+        w_front = [pool.tile([P, 2, HALF_M * PACK], BF16, name=f"w_front{h}", align_bytes=64) for h in range(2)]
+        w_back = pool.tile([P, 2, P * PACK], BF16, name="w_back", align_bytes=64)
 
-        def deal_source(u, h):
+        def deal_source(h, u):
             return w_raw[h][:].rearrange("p j (m t) -> p m j t", t=PACK)[:, :, :, 2 * u : 2 * u + 2]
 
-        def quantize_w(src, c0, width, scales):
-            nc.vector.quantize_mx(
-                out=w_codes[:, c0 : c0 + width].bitcast(FP8X4),
-                scales=scales,
-                in_=src,
-            )
+        def dealt(tile):
+            return tile[:].rearrange("p t (m j) -> p m j t", j=PACK)
 
-        w_front = [
-            reused.tile([P, P * PACK], BF16, name=f"w_front{h}", align_bytes=64, offset=h * P * PACK * 2) for h in range(2)
-        ]
-        w_back = pool.tile([P, 2 * P * PACK], BF16, name="w_back", align_bytes=64)
+        def quantize_w(src, c0, c1):
+            nc.vector.quantize_mx(out=w_codes[:, c0:c1].bitcast(FP8X4), scales=w_scales[:, c0:c1], in_=src)
 
-        def dealt(dst):
-            return dst.rearrange("p (t m j) -> p m j t", t=2, j=PACK)
+        def quantize_front(h, t):
+            quantize_w(w_front[h][:, t, :], t * P + h * HALF_M, t * P + (h + 1) * HALF_M)
 
-        nc.scalar.copy(out=dealt(w_front[0][:]), in_=deal_source(0, 0))
-        nc.scalar.copy(out=dealt(w_back[:])[:, 0:half_m, :, :], in_=deal_source(1, 0))
-        nc.scalar.copy(out=dealt(w_front[1][:]), in_=deal_source(0, 1))
-        quantize_w(w_front[0][:], 0, P, front_scales[:, 0:P])
-        x_scales = reused.tile([P, S], U8, name="x_scales", align_bytes=64, offset=0)
-        quantize_x(0, 0, HALF_S)
-        quantize_x(1, 0, P)
-        quantize_x(1, P, HALF_S)
-        nc.vector.tensor_copy(out=dealt(w_back[:])[:, half_m:, :, :], in_=deal_source(1, 1))
-        quantize_w(w_front[1][:], P, P, front_scales[:, P:])
-        back_scales = reused.tile([P, HALF_N], U8, name="back_scales", align_bytes=64, offset=8192 + 4096)
-        quantize_w(w_back[:], 2 * P, 2 * P, back_scales[:])
-        rest_sb = reused.tile([P, V], F32, name="rest_sb", align_bytes=64, offset=4096 + 2048)
+        nc.scalar.copy(out=dealt(w_front[0]), in_=deal_source(0, 0))
+        nc.scalar.copy(out=dealt(w_back)[:, 0:HALF_M], in_=deal_source(0, 1))
+        for t in range(2):
+            quantize_front(0, t)
+        nc.vector.tensor_copy(out=dealt(w_front[1]), in_=deal_source(1, 0))
+        nc.scalar.copy(out=dealt(w_back)[:, HALF_M:], in_=deal_source(1, 1))
+        rest_sb = pool.tile([P, V], F32, name="rest_sb")
         nc.vector.tensor_scalar(rest_sb[:], frac_sb[:], -1.0, 1.0, MULT, ADD)
+        for t in range(2):
+            quantize_front(1, t)
+        quantize_w(w_back[:].rearrange("p t c -> p (t c)"), 2 * P, N)
 
         y = [pool.tile([P, S], F32, name=f"y{t}") for t in range(PACK)]
 
-        def product(t, acc, cols):
+        def product(t, acc, picked):
             rows = slice(t * P, (t + 1) * P)
             nc.tensor.matmul_mx(
                 out=acc,
                 lhsT=w_codes[:, rows].bitcast(FP8X4),
-                lhsT_scale=(front_scales, back_scales)[t // 2][:, (t % 2) * P : (t % 2 + 1) * P],
-                rhs=x_codes[:, cols].bitcast(FP8X4),
-                rhs_scale=x_scales[:, cols],
+                lhsT_scale=w_scales[:, rows],
+                rhs=x_codes[:, picked].bitcast(FP8X4),
+                rhs_scale=x_scales[:, picked],
                 start=True,
                 stop=True,
             )
@@ -149,19 +141,16 @@ def tile_picked_lerp_none_lo_kernel(
         for i in range(PACK):
             product(0, first[i][:], slice(i * P, (i + 1) * P))
         for i in range(PACK):
-            nc.scalar.copy(out=y[0][:, i * P : (i + 1) * P], in_=first[i][:])
-        acc = {t: psum.tile([P, S], F32, name=f"acc{t}") for t in (1, 3, 2)}
+            copy_out = nc.scalar.copy if i % 2 == 0 else nc.vector.tensor_copy
+            copy_out(out=y[0][:, i * P : (i + 1) * P], in_=first[i][:])
+        acc = {t: psum.tile([P, S], F32, name=f"acc{t}") for t in range(1, PACK)}
         for t in acc:
             product(t, acc[t][:], slice(0, S))
-        for t, cols in ((1, slice(0, S)), (3, slice(0, HALF_S)), (2, slice(0, S)), (3, slice(HALF_S, S))):
-            nc.scalar.copy(out=y[t][:, cols], in_=acc[t][:, cols])
-
-        rest_col = pool.tile([P, 2], F32, name="rest_col")
-        nc.scalar.activation(out=rest_col[:], in_=frac_col[:], func=COPY, bias=1.0, scale=-1.0)
 
         last = PACK - 1
-        left_part = pool.tile([P, 2, V], F32, name="left_part")
-        right_part = pool.tile([P, 2, V], F32, name="right_part")
+        left_found = [pool.tile([P, V], F32, name=f"left_found{t}") for t in range(PACK)]
+        left_part = [pool.tile([P, V], F32, name=f"left_part{t}") for t in range(PACK)]
+        right_part = [pool.tile([P, V], F32, name=f"right_part{t}") for t in range(PACK)]
         result = pool.tile([P, PACK, V], F32, name="result")
         pieces = ((0, SCALAR_ROUNDS), (SCALAR_ROUNDS, HALF_V), (HALF_V, V))
         rounded = [pool.tile([P, v1 - v0, PACK], BF16, name=f"rounded{v0}", align_bytes=64) for v0, v1 in pieces]
@@ -172,54 +161,18 @@ def tile_picked_lerp_none_lo_kernel(
         def v_cols(h):
             return slice(h * HALF_V, (h + 1) * HALF_V)
 
-        weighted = [pool.tile([P, 2, 2, P], F32, name=f"weighted{i}") for i in range(2)]
-
-        founds = [pool.tile([P, V], F32, name=f"found{n}") for n in range(4)]
-
-        def weigh_turned(a, banks):
-            for i, (places, factor) in enumerate(((right_sb, frac_col), (left_sb, rest_col))):
-                found = founds[2 * a + i]
-                nc.vector.tensor_copy(out=found[:], in_=y[a][:].indirect(places[:]))
-                turned = psum.tile([P, 2, P], F32, name=f"turned{i}{a}", tag=banks[i])
-                for h in range(2):
-                    nc.tensor.transpose(turned[:, h, :], found[:, v_cols(h)], identity[:])
-                for h in range(2):
-                    nc.scalar.activation(
-                        out=weighted[i][:, h, :, a * half_m : (a + 1) * half_m],
-                        in_=turned[:, h, :].rearrange("p (t m) -> p t m", t=2),
-                        func=COPY,
-                        scale=factor[:, h : h + 1],
-                    )
-
-        weigh_turned(0, ("first0", "first1"))
-        weigh_turned(1, ("first2", "first3"))
-        summed = psum.tile([P, 2, V], F32, name="summed")
-        turns = [(i, h, t) for i in range(2) for h in range(2) for t in range(2)]
-        for i, h, t in turns:
-            nc.tensor.matmul(
-                summed[:, t, v_cols(h)],
-                weighted[i][:, h, t, :],
-                identity[:],
-                start=(i, h, t) == turns[0],
-                stop=(i, h, t) == turns[-1],
-                is_transpose=True,
-            )
-        nc.scalar.copy(out=result[:, 0:2, :], in_=summed[:])
-        nc.scalar.dma_start(out=out_rows[:, 0:2, :], in_=result[:, 0:2, :])
-
-        nc.vector.tensor_tensor(left_part[:, 0, :], y[2][:].indirect(left_sb[:]), rest_sb[:], MULT)
-        nc.vector.tensor_tensor(right_part[:, 0, :], y[2][:].indirect(right_sb[:]), frac_sb[:], MULT)
-
-        def gather_last(dst, places, factor, h):
-            cols = HALF_V // 16
-            nc.vector.tensor_tensor(
-                dst[:, 1, v_cols(h)], y[last][:].indirect(places[:, h * cols : (h + 1) * cols]), factor[:, v_cols(h)], MULT
-            )
-
-        def add_parts(h):
-            nc.vector.tensor_tensor(
-                result[:, last, v_cols(h)], left_part[:, 1, v_cols(h)], right_part[:, 1, v_cols(h)], ADD
-            )
+        for t in range(PACK):
+            if t < last:
+                nc.scalar.copy(out=y[t + 1][:], in_=acc[t + 1][:])
+            nc.scalar.activation(left_found[t][:], y[t][:].indirect(left_sb[:]), COPY)
+            nc.vector.tensor_tensor(right_part[t][:], y[t][:].indirect(right_sb[:]), frac_sb[:], MULT)
+            nc.vector.tensor_tensor(left_part[t][:], left_found[t][:], rest_sb[:], MULT)
+            if t < last:
+                nc.vector.tensor_tensor(result[:, t, :], left_part[t][:], right_part[t][:], ADD)
+            if t == 1:
+                nc.sync.dma_start(out=out_rows[:, 0:2, :], in_=result[:, 0:2, :])
+            if t == 2:
+                nc.sync.dma_start(out=out_rows[:, 2, :], in_=result[:, 2, :])
 
         def round_views(i):
             dst = rounded[i][:].rearrange("p (c n) t -> p c t n", n=PACK)
@@ -232,14 +185,11 @@ def tile_picked_lerp_none_lo_kernel(
                 in_=rounded[i][:].rearrange("p v t -> p (v t)"),
             )
 
-        nc.vector.tensor_tensor(left_part[:, 1, :], y[last][:].indirect(left_sb[:]), rest_sb[:], MULT)
-        nc.vector.tensor_tensor(result[:, 2, :], left_part[:, 0, :], right_part[:, 0, :], ADD)
-        nc.sync.dma_start(out=out_rows[:, 2, :], in_=result[:, 2, :])
-        gather_last(right_part, right_sb, frac_sb, 0)
-        gather_last(right_part, right_sb, frac_sb, 1)
-        add_parts(0)
+        for h in range(2):
+            nc.vector.tensor_tensor(
+                result[:, last, v_cols(h)], left_part[last][:, v_cols(h)], right_part[last][:, v_cols(h)], ADD
+            )
         nc.scalar.copy(*round_views(0))
-        add_parts(1)
         nc.sync.dma_start(out=out_rows[:, last, :], in_=result[:, last, :])
         nc.vector.tensor_copy(*round_views(1))
         nc.vector.tensor_copy(*round_views(2))

@@ -1,6 +1,7 @@
 from contextlib import ExitStack
 
 import concourse.mybir as mybir
+from concourse.masks import make_identity
 
 K, T, S, V, N = 512, 1024, 512, 256, 512
 FLOPS = 2 * K * N * S
@@ -58,41 +59,41 @@ def tile_picked_lerp_none_lo_kernel(
         nc.gpsimd.memset(idle[:, 0:1], 0.0)
         nc.scalar.copy(out=idle[:, 1:2], in_=idle[:, 0:1])
 
-        x_found = [[pool.tile([P, 2, HALF_S], F32, name=f"x_found{u}{h}") for h in range(2)] for u in range(2)]
-        x_pieces = ((0, HALF_S), (HALF_S, HALF_S + P), (HALF_S + P, S))
-        x_picked = [pool.tile([P, s1 - s0, PACK], BF16, name=f"x_picked{s0}", align_bytes=64) for s0, s1 in x_pieces]
+        identity = pool.tile([P, P], F32, name="identity")
+        make_identity(nc, identity[:])
+
+        x_found = [{i: pool.tile([P, 2, P], F32, name=f"x_found{u}{i}") for i in (2, 3)} for u in range(2)]
+        x_picked = [pool.tile([P, P, PACK], BF16, name=f"x_picked{i}", align_bytes=64) for i in range(PACK)]
         x_codes = pool.tile([P, S], U32, name="x_codes", align_bytes=64)
         x_scales = pool.tile([P, S], U8, name="x_scales", align_bytes=64)
 
         def weave_views(u, i):
-            s0, s1 = x_pieces[i]
-            h = s0 // HALF_S
-            src = x_found[u][h][:, :, s0 - h * HALF_S : s1 - h * HALF_S].rearrange("p j s -> p s j")
-            return x_picked[i][:, :, 2 * u : 2 * u + 2], src
+            return x_picked[i][:, :, 2 * u : 2 * u + 2], x_found[u][i][:].rearrange("p j s -> p s j")
 
-        def pick_views(j, s0, s1):
-            h = s0 // HALF_S
-            dst = x_found[j // 2][h][:, j % 2, s0 - h * HALF_S : s1 - h * HALF_S]
-            return dst, x_raw[j][:].indirect(offs_sb[:, s0 // 16 : s1 // 16])
+        def picked_by(j, i):
+            cols = P // 16
+            return x_raw[j][:].indirect(offs_sb[:, i * cols : (i + 1) * cols])
 
         for j in range(PACK):
-            border = P if j == 2 else HALF_S
-            nc.vector.tensor_copy(*pick_views(j, 0, border))
-            if border < HALF_S:
-                nc.scalar.activation(*pick_views(j, border, HALF_S), COPY)
-            nc.scalar.activation(*pick_views(j, HALF_S, S), COPY)
+            for i in (0, 1):
+                nc.vector.tensor_copy(out=x_picked[i][:, :, j], in_=picked_by(j, i))
+            for i in (2, 3):
+                nc.scalar.activation(x_found[j // 2][i][:, j % 2, :], picked_by(j, i), COPY)
             if j == 1:
-                for i in range(3):
-                    nc.vector.tensor_copy(*weave_views(0, i))
-        nc.vector.tensor_copy(*weave_views(1, 0))
-        nc.scalar.copy(*weave_views(1, 1))
-        nc.vector.tensor_copy(*weave_views(1, 2))
-        for i, (s0, s1) in enumerate(x_pieces):
+                nc.scalar.copy(*weave_views(0, 2))
+                nc.vector.tensor_copy(*weave_views(0, 3))
+
+        def quantize_x(i):
             nc.vector.quantize_mx(
-                out=x_codes[:, s0:s1].bitcast(FP8X4),
-                scales=x_scales[:, s0:s1],
+                out=x_codes[:, i * P : (i + 1) * P].bitcast(FP8X4),
+                scales=x_scales[:, i * P : (i + 1) * P],
                 in_=x_picked[i][:].rearrange("p s j -> p (s j)"),
             )
+
+        nc.scalar.copy(*weave_views(1, 2))
+        quantize_x(0)
+        nc.vector.tensor_copy(*weave_views(1, 3))
+        quantize_x(1)
 
         w_codes = pool.tile([P, N], U32, name="w_codes", align_bytes=64)
         w_scales = pool.tile([P, N], U8, name="w_scales", align_bytes=64)
@@ -106,22 +107,22 @@ def tile_picked_lerp_none_lo_kernel(
             return tile[:].rearrange("p t (m j) -> p m j t", j=PACK)
 
         def quantize_w(src, c0, c1):
-            nc.vector.quantize_mx(out=w_codes[:, c0:c1].bitcast(FP8X4), scales=w_scales[:, c0:c1], in_=src)
-
-        def quantize_front(h, t):
-            quantize_w(w_front[h][:, t, :], t * P + h * HALF_M, t * P + (h + 1) * HALF_M)
+            nc.vector.quantize_mx(
+                out=w_codes[:, c0:c1].bitcast(FP8X4),
+                scales=w_scales[:, c0:c1],
+                in_=src[:].rearrange("p t c -> p (t c)"),
+            )
 
         nc.scalar.copy(out=dealt(w_front[0]), in_=deal_source(0, 0))
+        quantize_x(2)
+        quantize_x(3)
+        quantize_w(w_front[0], 0, P)
         nc.scalar.copy(out=dealt(w_back)[:, 0:HALF_M], in_=deal_source(0, 1))
-        for t in range(2):
-            quantize_front(0, t)
         nc.vector.tensor_copy(out=dealt(w_front[1]), in_=deal_source(1, 0))
-        nc.scalar.copy(out=dealt(w_back)[:, HALF_M:], in_=deal_source(1, 1))
+        nc.vector.tensor_copy(out=dealt(w_back)[:, HALF_M:], in_=deal_source(1, 1))
+        quantize_w(w_front[1], P, 2 * P)
+        quantize_w(w_back, 2 * P, N)
         rest_sb = pool.tile([P, V], F32, name="rest_sb")
-        nc.vector.tensor_scalar(rest_sb[:], frac_sb[:], -1.0, 1.0, MULT, ADD)
-        for t in range(2):
-            quantize_front(1, t)
-        quantize_w(w_back[:].rearrange("p t c -> p (t c)"), 2 * P, N)
 
         y = [pool.tile([P, S], F32, name=f"y{t}") for t in range(PACK)]
 
@@ -141,15 +142,18 @@ def tile_picked_lerp_none_lo_kernel(
         for i in range(PACK):
             product(0, first[i][:], slice(i * P, (i + 1) * P))
         for i in range(PACK):
-            copy_out = nc.scalar.copy if i % 2 == 0 else nc.vector.tensor_copy
-            copy_out(out=y[0][:, i * P : (i + 1) * P], in_=first[i][:])
+            nc.scalar.copy(out=y[0][:, i * P : (i + 1) * P], in_=first[i][:])
+        nc.vector.tensor_scalar(rest_sb[:], frac_sb[:], -1.0, 1.0, MULT, ADD)
         acc = {t: psum.tile([P, S], F32, name=f"acc{t}") for t in range(1, PACK)}
         for t in acc:
             product(t, acc[t][:], slice(0, S))
+        for t in acc:
+            nc.scalar.copy(out=y[t][:], in_=acc[t][:])
 
         last = PACK - 1
-        left_found = [pool.tile([P, V], F32, name=f"left_found{t}") for t in range(PACK)]
+        left_found = {2: pool.tile([P, V], F32, name="left_found2")}
         left_part = [pool.tile([P, V], F32, name=f"left_part{t}") for t in range(PACK)]
+        left_found[3] = left_part[1]
         right_part = [pool.tile([P, V], F32, name=f"right_part{t}") for t in range(PACK)]
         result = pool.tile([P, PACK, V], F32, name="result")
         pieces = ((0, SCALAR_ROUNDS), (SCALAR_ROUNDS, HALF_V), (HALF_V, V))
@@ -161,18 +165,46 @@ def tile_picked_lerp_none_lo_kernel(
         def v_cols(h):
             return slice(h * HALF_V, (h + 1) * HALF_V)
 
-        for t in range(PACK):
-            if t < last:
-                nc.scalar.copy(out=y[t + 1][:], in_=acc[t + 1][:])
-            nc.scalar.activation(left_found[t][:], y[t][:].indirect(left_sb[:]), COPY)
+        regrouped = pool.tile([P, 2, 2, P], F32, name="regrouped")
+
+        def weigh_right(t):
             nc.vector.tensor_tensor(right_part[t][:], y[t][:].indirect(right_sb[:]), frac_sb[:], MULT)
-            nc.vector.tensor_tensor(left_part[t][:], left_found[t][:], rest_sb[:], MULT)
-            if t < last:
-                nc.vector.tensor_tensor(result[:, t, :], left_part[t][:], right_part[t][:], ADD)
-            if t == 1:
-                nc.sync.dma_start(out=out_rows[:, 0:2, :], in_=result[:, 0:2, :])
-            if t == 2:
-                nc.sync.dma_start(out=out_rows[:, 2, :], in_=result[:, 2, :])
+
+        def weigh_left(t):
+            nc.vector.tensor_tensor(left_part[t][:], y[t][:].indirect(left_sb[:]), rest_sb[:], MULT)
+
+        def turn_sum(a):
+            turned = psum.tile([P, 2, P], F32, name=f"turned{a}", tag=f"first{a}")
+            for h in range(2):
+                for i, part in enumerate((right_part[a], left_part[a])):
+                    nc.tensor.matmul(
+                        turned[:, h, :], part[:, v_cols(h)], identity[:], start=i == 0, stop=i == 1, is_transpose=True
+                    )
+            nc.scalar.copy(
+                out=regrouped[:, :, :, a * HALF_M : (a + 1) * HALF_M],
+                in_=turned[:].rearrange("p h (t m) -> p h t m", t=2),
+            )
+
+        weigh_right(0)
+        weigh_left(0)
+        turn_sum(0)
+        weigh_right(1)
+        weigh_left(1)
+        nc.scalar.activation(left_found[2][:], y[2][:].indirect(left_sb[:]), COPY)
+        turn_sum(1)
+        summed = psum.tile([P, 2, V], F32, name="summed", tag="first2")
+        for h in range(2):
+            for t in range(2):
+                nc.tensor.transpose(summed[:, t, v_cols(h)], regrouped[:, h, t, :], identity[:])
+        weigh_right(2)
+        weigh_right(3)
+        nc.vector.tensor_tensor(left_part[2][:], left_found[2][:], rest_sb[:], MULT)
+        nc.scalar.activation(left_found[3][:], y[3][:].indirect(left_sb[:]), COPY)
+        nc.scalar.copy(out=result[:, 0:2, :], in_=summed[:])
+        nc.sync.dma_start(out=out_rows[:, 0:2, :], in_=result[:, 0:2, :])
+        nc.vector.tensor_tensor(result[:, 2, :], left_part[2][:], right_part[2][:], ADD)
+        nc.sync.dma_start(out=out_rows[:, 2, :], in_=result[:, 2, :])
+        nc.vector.tensor_tensor(left_part[3][:], left_found[3][:], rest_sb[:], MULT)
 
         def round_views(i):
             dst = rounded[i][:].rearrange("p (c n) t -> p c t n", n=PACK)

@@ -23,7 +23,6 @@ HALF_S = S // 2
 HALF_N = N // 2
 HALF_M = P // 2
 HALF_V = V // 2
-SCALAR_ROUNDS = 64
 
 
 def tile_picked_lerp_none_lo_kernel(
@@ -51,9 +50,9 @@ def tile_picked_lerp_none_lo_kernel(
             nc.sync.dma_start(out=x_raw[j][:], in_=x_rows[:, j, :])
         for h in range(2):
             nc.sync.dma_start(out=w_raw[h][:], in_=w_rows[:, :, h * HALF_N : (h + 1) * HALF_N])
+        nc.sync.dma_start(out=frac_sb[:], in_=frac)
         nc.sync.dma_start(right_sb[:], right)
         nc.sync.dma_start(left_sb[:], left)
-        nc.sync.dma_start(out=frac_sb[:], in_=frac)
 
         idle = pool.tile([P, 2], F32, name="idle")
         nc.gpsimd.memset(idle[:, 0:1], 0.0)
@@ -143,7 +142,7 @@ def tile_picked_lerp_none_lo_kernel(
             product(0, first[i][:], slice(i * P, (i + 1) * P))
         for i in range(PACK):
             nc.scalar.copy(out=y[0][:, i * P : (i + 1) * P], in_=first[i][:])
-        nc.vector.tensor_scalar(rest_sb[:], frac_sb[:], -1.0, 1.0, MULT, ADD)
+        nc.scalar.activation(out=rest_sb[:], in_=frac_sb[:], func=COPY, bias=1.0, scale=-1.0)
         acc = {t: psum.tile([P, S], F32, name=f"acc{t}") for t in range(1, PACK)}
         for t in acc:
             product(t, acc[t][:], slice(0, S))
@@ -153,11 +152,9 @@ def tile_picked_lerp_none_lo_kernel(
         last = PACK - 1
         left_found = {2: pool.tile([P, V], F32, name="left_found2")}
         left_part = [pool.tile([P, V], F32, name=f"left_part{t}") for t in range(PACK)]
-        left_found[3] = left_part[1]
         right_part = [pool.tile([P, V], F32, name=f"right_part{t}") for t in range(PACK)]
         result = pool.tile([P, PACK, V], F32, name="result")
-        pieces = ((0, SCALAR_ROUNDS), (SCALAR_ROUNDS, HALF_V), (HALF_V, V))
-        rounded = [pool.tile([P, v1 - v0, PACK], BF16, name=f"rounded{v0}", align_bytes=64) for v0, v1 in pieces]
+        rounded = [pool.tile([P, HALF_V, PACK], BF16, name=f"rounded{h}", align_bytes=64) for h in range(2)]
         o_codes = pool.tile([P, V], U32, name="o_codes", align_bytes=64)
         o_scales = pool.tile([P, V], U8, name="o_scales", align_bytes=64)
         out_rows = out_0.rearrange("(p t) v -> p t v", t=PACK)
@@ -165,7 +162,7 @@ def tile_picked_lerp_none_lo_kernel(
         def v_cols(h):
             return slice(h * HALF_V, (h + 1) * HALF_V)
 
-        regrouped = pool.tile([P, 2, 2, P], F32, name="regrouped")
+        regrouped = [pool.tile([P, 2, P], F32, name=f"regrouped{h}") for h in range(2)]
 
         def weigh_right(t):
             nc.vector.tensor_tensor(right_part[t][:], y[t][:].indirect(right_sb[:]), frac_sb[:], MULT)
@@ -173,60 +170,57 @@ def tile_picked_lerp_none_lo_kernel(
         def weigh_left(t):
             nc.vector.tensor_tensor(left_part[t][:], y[t][:].indirect(left_sb[:]), rest_sb[:], MULT)
 
-        def turn_sum(a):
-            turned = psum.tile([P, 2, P], F32, name=f"turned{a}", tag=f"first{a}")
+        turned = [psum.tile([P, 2, P], F32, name=f"turned{h}", tag=f"first{h}") for h in range(2)]
+
+        def turn(a, part, start=False, stop=False):
             for h in range(2):
-                for i, part in enumerate((right_part[a], left_part[a])):
-                    nc.tensor.matmul(
-                        turned[:, h, :], part[:, v_cols(h)], identity[:], start=i == 0, stop=i == 1, is_transpose=True
-                    )
-            nc.scalar.copy(
-                out=regrouped[:, :, :, a * HALF_M : (a + 1) * HALF_M],
-                in_=turned[:].rearrange("p h (t m) -> p h t m", t=2),
-            )
+                nc.tensor.matmul(
+                    turned[h][:, a, :], part[:, v_cols(h)], identity[:], start=start, stop=stop, is_transpose=True
+                )
 
         weigh_right(0)
         weigh_left(0)
-        turn_sum(0)
+        turn(0, right_part[0], start=True)
+        turn(0, left_part[0])
         weigh_right(1)
         weigh_left(1)
         nc.scalar.activation(left_found[2][:], y[2][:].indirect(left_sb[:]), COPY)
-        turn_sum(1)
-        summed = psum.tile([P, 2, V], F32, name="summed", tag="first2")
+        turn(1, right_part[1])
+        turn(1, left_part[1], stop=True)
+        for h in range(2):
+            nc.scalar.copy(
+                out=regrouped[h][:].rearrange("p t (a m) -> p t a m", a=2),
+                in_=turned[h][:].rearrange("p a (t m) -> p t a m", t=2),
+            )
+        summed = [psum.tile([P, 2, HALF_V], F32, name=f"summed{h}", tag=f"first{2 + h}") for h in range(2)]
         for h in range(2):
             for t in range(2):
-                nc.tensor.transpose(summed[:, t, v_cols(h)], regrouped[:, h, t, :], identity[:])
+                nc.tensor.transpose(summed[h][:, t, :], regrouped[h][:, t, :], identity[:])
         weigh_right(2)
         weigh_right(3)
         nc.vector.tensor_tensor(left_part[2][:], left_found[2][:], rest_sb[:], MULT)
-        nc.scalar.activation(left_found[3][:], y[3][:].indirect(left_sb[:]), COPY)
-        nc.scalar.copy(out=result[:, 0:2, :], in_=summed[:])
+        weigh_left(3)
+        for h in range(2):
+            nc.scalar.copy(out=result[:, 0:2, v_cols(h)], in_=summed[h][:])
         nc.sync.dma_start(out=out_rows[:, 0:2, :], in_=result[:, 0:2, :])
+        for h in range(2):
+            nc.scalar.copy(out=rounded[h][:, :, 0:2], in_=summed[h][:].rearrange("p t v -> p v t"))
         nc.vector.tensor_tensor(result[:, 2, :], left_part[2][:], right_part[2][:], ADD)
         nc.sync.dma_start(out=out_rows[:, 2, :], in_=result[:, 2, :])
-        nc.vector.tensor_tensor(left_part[3][:], left_found[3][:], rest_sb[:], MULT)
-
-        def round_views(i):
-            dst = rounded[i][:].rearrange("p (c n) t -> p c t n", n=PACK)
-            return dst, result[:, :, slice(*pieces[i])].rearrange("p t (c n) -> p c t n", n=PACK)
-
-        def quantize_result(i):
-            nc.vector.quantize_mx(
-                out=o_codes[:, slice(*pieces[i])].bitcast(FP8X4),
-                scales=o_scales[:, slice(*pieces[i])],
-                in_=rounded[i][:].rearrange("p v t -> p (v t)"),
-            )
 
         for h in range(2):
             nc.vector.tensor_tensor(
                 result[:, last, v_cols(h)], left_part[last][:, v_cols(h)], right_part[last][:, v_cols(h)], ADD
             )
-        nc.scalar.copy(*round_views(0))
         nc.sync.dma_start(out=out_rows[:, last, :], in_=result[:, last, :])
-        nc.vector.tensor_copy(*round_views(1))
-        nc.vector.tensor_copy(*round_views(2))
-        for i in (1, 0, 2):
-            quantize_result(i)
+        for h in range(2):
+            nc.vector.tensor_copy(out=rounded[h][:, :, 2:4], in_=result[:, 2:4, v_cols(h)].rearrange("p t v -> p v t"))
+        for h in range(2):
+            nc.vector.quantize_mx(
+                out=o_codes[:, v_cols(h)].bitcast(FP8X4),
+                scales=o_scales[:, v_cols(h)],
+                in_=rounded[h][:].rearrange("p v t -> p (v t)"),
+            )
 
         nc.sync.dma_start(
             out=out_1.rearrange("z p c r -> p (z c r)").bitcast(I32), in_=o_codes[:].bitcast(I32)

@@ -149,7 +149,6 @@ def tile_picked_lerp_none_lo_kernel(
         for t in acc:
             nc.scalar.copy(out=y[t][:], in_=acc[t][:])
 
-        last = PACK - 1
         left_found = {2: pool.tile([P, V], F32, name="left_found2")}
         left_part = [pool.tile([P, V], F32, name=f"left_part{t}") for t in range(PACK)]
         right_part = [pool.tile([P, V], F32, name=f"right_part{t}") for t in range(PACK)]
@@ -198,21 +197,20 @@ def tile_picked_lerp_none_lo_kernel(
                 nc.tensor.transpose(summed[h][:, t, :], regrouped[h][:, t, :], identity[:])
         weigh_right(2)
         weigh_right(3)
-        nc.vector.tensor_tensor(left_part[2][:], left_found[2][:], rest_sb[:], MULT)
         weigh_left(3)
+        nc.vector.tensor_tensor(left_part[2][:], left_found[2][:], rest_sb[:], MULT)
         for h in range(2):
             nc.scalar.copy(out=result[:, 0:2, v_cols(h)], in_=summed[h][:])
         nc.sync.dma_start(out=out_rows[:, 0:2, :], in_=result[:, 0:2, :])
         for h in range(2):
             nc.scalar.copy(out=rounded[h][:, :, 0:2], in_=summed[h][:].rearrange("p t v -> p v t"))
-        nc.vector.tensor_tensor(result[:, 2, :], left_part[2][:], right_part[2][:], ADD)
-        nc.sync.dma_start(out=out_rows[:, 2, :], in_=result[:, 2, :])
-
+        nc.vector.tensor_tensor(result[:, 3, :], left_part[3][:], right_part[3][:], ADD)
+        nc.sync.dma_start(out=out_rows[:, 3, :], in_=result[:, 3, :])
         for h in range(2):
             nc.vector.tensor_tensor(
-                result[:, last, v_cols(h)], left_part[last][:, v_cols(h)], right_part[last][:, v_cols(h)], ADD
+                result[:, 2, v_cols(h)], left_part[2][:, v_cols(h)], right_part[2][:, v_cols(h)], ADD
             )
-        nc.sync.dma_start(out=out_rows[:, last, :], in_=result[:, last, :])
+        nc.sync.dma_start(out=out_rows[:, 2, :], in_=result[:, 2, :])
         for h in range(2):
             nc.vector.tensor_copy(out=rounded[h][:, :, 2:4], in_=result[:, 2:4, v_cols(h)].rearrange("p t v -> p v t"))
         for h in range(2):

@@ -96,32 +96,29 @@ def tile_picked_lerp_none_lo_kernel(
 
         w_codes = pool.tile([P, N], U32, name="w_codes", align_bytes=64)
         w_scales = pool.tile([P, N], U8, name="w_scales", align_bytes=64)
-        w_front = [pool.tile([P, 2, HALF_M * PACK], BF16, name=f"w_front{h}", align_bytes=64) for h in range(2)]
-        w_back = pool.tile([P, 2, P * PACK], BF16, name="w_back", align_bytes=64)
+        w_first = pool.tile([P, 2, HALF_M * PACK], BF16, name="w_first", align_bytes=64)
+        w_dealt = pool.tile([P, PACK, P * PACK], BF16, name="w_dealt", align_bytes=64)
 
-        def deal_source(h, u):
-            return w_raw[h][:].rearrange("p j (m t) -> p m j t", t=PACK)[:, :, :, 2 * u : 2 * u + 2]
+        def deal_source(h):
+            return w_raw[h][:].rearrange("p j (m t) -> p m j t", t=PACK)
 
         def dealt(tile):
             return tile[:].rearrange("p t (m j) -> p m j t", j=PACK)
 
         def quantize_w(src, c0, c1):
-            nc.vector.quantize_mx(
-                out=w_codes[:, c0:c1].bitcast(FP8X4),
-                scales=w_scales[:, c0:c1],
-                in_=src[:].rearrange("p t c -> p (t c)"),
-            )
+            nc.vector.quantize_mx(out=w_codes[:, c0:c1].bitcast(FP8X4), scales=w_scales[:, c0:c1], in_=src)
 
-        nc.scalar.copy(out=dealt(w_front[0]), in_=deal_source(0, 0))
+        nc.scalar.copy(out=dealt(w_first), in_=deal_source(0)[:, :, :, 0:2])
         quantize_x(2)
         quantize_x(3)
-        quantize_w(w_front[0], 0, P)
-        nc.scalar.copy(out=dealt(w_back)[:, 0:HALF_M], in_=deal_source(0, 1))
-        nc.vector.tensor_copy(out=dealt(w_front[1]), in_=deal_source(1, 0))
-        nc.vector.tensor_copy(out=dealt(w_back)[:, HALF_M:], in_=deal_source(1, 1))
-        quantize_w(w_front[1], P, 2 * P)
-        quantize_w(w_back, 2 * P, N)
+        quantize_w(w_first[:].rearrange("p t c -> p (t c)"), 0, P)
+        nc.scalar.copy(out=dealt(w_dealt)[:, 0:HALF_M, :, 2:4], in_=deal_source(0)[:, :, :, 2:4])
+        nc.vector.tensor_copy(out=dealt(w_dealt)[:, HALF_M:], in_=deal_source(1))
         rest_sb = pool.tile([P, V], F32, name="rest_sb")
+        nc.vector.tensor_scalar(rest_sb[:], frac_sb[:], -1.0, 1.0, MULT, ADD)
+        for t in range(2):
+            quantize_w(w_dealt[:, t, HALF_M * PACK :], P + t * HALF_M, P + (t + 1) * HALF_M)
+        quantize_w(w_dealt[:, 2:4, :].rearrange("p t c -> p (t c)"), 2 * P, N)
 
         y = [pool.tile([P, S], F32, name=f"y{t}") for t in range(PACK)]
 
@@ -142,10 +139,14 @@ def tile_picked_lerp_none_lo_kernel(
             product(0, first[i][:], slice(i * P, (i + 1) * P))
         for i in range(PACK):
             nc.scalar.copy(out=y[0][:, i * P : (i + 1) * P], in_=first[i][:])
-        nc.scalar.activation(out=rest_sb[:], in_=frac_sb[:], func=COPY, bias=1.0, scale=-1.0)
-        acc = {t: psum.tile([P, S], F32, name=f"acc{t}") for t in range(1, PACK)}
+        second = [psum.tile([P, HALF_S], F32, name=f"second{h}") for h in range(2)]
+        acc = {t: psum.tile([P, S], F32, name=f"acc{t}") for t in (2, 3)}
+        for h in range(2):
+            product(1, second[h][:], slice(h * HALF_S, (h + 1) * HALF_S))
         for t in acc:
             product(t, acc[t][:], slice(0, S))
+        for h in range(2):
+            nc.scalar.copy(out=y[1][:, h * HALF_S : (h + 1) * HALF_S], in_=second[h][:])
         for t in acc:
             nc.scalar.copy(out=y[t][:], in_=acc[t][:])
 

@@ -150,7 +150,7 @@ def tile_picked_lerp_none_lo_kernel(
         for t in acc:
             nc.scalar.copy(out=y[t][:], in_=acc[t][:])
 
-        left_found = {2: pool.tile([P, V], F32, name="left_found2")}
+        left_found = {t: pool.tile([P, V], F32, name=f"left_found{t}") for t in (2, 3)}
         left_part = [pool.tile([P, V], F32, name=f"left_part{t}") for t in range(PACK)]
         right_part = [pool.tile([P, V], F32, name=f"right_part{t}") for t in range(PACK)]
         result = pool.tile([P, PACK, V], F32, name="result")
@@ -184,7 +184,8 @@ def tile_picked_lerp_none_lo_kernel(
         turn(0, left_part[0])
         weigh_right(1)
         weigh_left(1)
-        nc.scalar.activation(left_found[2][:], y[2][:].indirect(left_sb[:]), COPY)
+        for t in (2, 3):
+            nc.scalar.activation(left_found[t][:], y[t][:].indirect(left_sb[:]), COPY)
         turn(1, right_part[1])
         turn(1, left_part[1], stop=True)
         for h in range(2):
@@ -198,22 +199,23 @@ def tile_picked_lerp_none_lo_kernel(
                 nc.tensor.transpose(summed[h][:, t, :], regrouped[h][:, t, :], identity[:])
         weigh_right(2)
         weigh_right(3)
-        weigh_left(3)
-        nc.vector.tensor_tensor(left_part[2][:], left_found[2][:], rest_sb[:], MULT)
+        for t in (2, 3):
+            nc.vector.tensor_tensor(left_part[t][:], left_found[t][:], rest_sb[:], MULT)
+        nc.vector.tensor_tensor(result[:, 2, :], left_part[2][:], right_part[2][:], ADD)
+        nc.sync.dma_start(out=out_rows[:, 2, :], in_=result[:, 2, :])
         for h in range(2):
             nc.scalar.copy(out=result[:, 0:2, v_cols(h)], in_=summed[h][:])
         nc.sync.dma_start(out=out_rows[:, 0:2, :], in_=result[:, 0:2, :])
         for h in range(2):
-            nc.scalar.copy(out=rounded[h][:, :, 0:2], in_=summed[h][:].rearrange("p t v -> p v t"))
-        nc.vector.tensor_tensor(result[:, 3, :], left_part[3][:], right_part[3][:], ADD)
+            nc.vector.tensor_tensor(
+                result[:, 3, v_cols(h)], left_part[3][:, v_cols(h)], right_part[3][:, v_cols(h)], ADD
+            )
         nc.sync.dma_start(out=out_rows[:, 3, :], in_=result[:, 3, :])
         for h in range(2):
-            nc.vector.tensor_tensor(
-                result[:, 2, v_cols(h)], left_part[2][:, v_cols(h)], right_part[2][:, v_cols(h)], ADD
+            nc.vector.tensor_copy(
+                out=rounded[h][:].rearrange("p (c i) t -> p c t i", i=PACK),
+                in_=result[:, :, v_cols(h)].rearrange("p t (c i) -> p c t i", i=PACK),
             )
-        nc.sync.dma_start(out=out_rows[:, 2, :], in_=result[:, 2, :])
-        for h in range(2):
-            nc.vector.tensor_copy(out=rounded[h][:, :, 2:4], in_=result[:, 2:4, v_cols(h)].rearrange("p t v -> p v t"))
         for h in range(2):
             nc.vector.quantize_mx(
                 out=o_codes[:, v_cols(h)].bitcast(FP8X4),

@@ -50,9 +50,9 @@ def tile_picked_lerp_none_lo_kernel(
             nc.sync.dma_start(out=x_raw[j][:], in_=x_rows[:, j, :])
         for h in range(2):
             nc.sync.dma_start(out=w_raw[h][:], in_=w_rows[:, :, h * HALF_N : (h + 1) * HALF_N])
-        nc.sync.dma_start(out=frac_sb[:], in_=frac)
         nc.sync.dma_start(right_sb[:], right)
         nc.sync.dma_start(left_sb[:], left)
+        nc.sync.dma_start(out=frac_sb[:], in_=frac)
 
         idle = pool.tile([P, 2], F32, name="idle")
         nc.gpsimd.memset(idle[:, 0:1], 0.0)
@@ -96,8 +96,8 @@ def tile_picked_lerp_none_lo_kernel(
 
         w_codes = pool.tile([P, N], U32, name="w_codes", align_bytes=64)
         w_scales = pool.tile([P, N], U8, name="w_scales", align_bytes=64)
-        w_first = pool.tile([P, 2, HALF_M * PACK], BF16, name="w_first", align_bytes=64)
-        w_dealt = pool.tile([P, PACK, P * PACK], BF16, name="w_dealt", align_bytes=64)
+        w_front = [pool.tile([P, 2, HALF_M * PACK], BF16, name=f"w_front{h}", align_bytes=64) for h in range(2)]
+        w_back = pool.tile([P, 2, P * PACK], BF16, name="w_back", align_bytes=64)
 
         def deal_source(h):
             return w_raw[h][:].rearrange("p j (m t) -> p m j t", t=PACK)
@@ -105,20 +105,24 @@ def tile_picked_lerp_none_lo_kernel(
         def dealt(tile):
             return tile[:].rearrange("p t (m j) -> p m j t", j=PACK)
 
-        def quantize_w(src, c0, c1):
-            nc.vector.quantize_mx(out=w_codes[:, c0:c1].bitcast(FP8X4), scales=w_scales[:, c0:c1], in_=src)
+        def quantize_w(tile, c0, c1):
+            nc.vector.quantize_mx(
+                out=w_codes[:, c0:c1].bitcast(FP8X4),
+                scales=w_scales[:, c0:c1],
+                in_=tile[:].rearrange("p t c -> p (t c)"),
+            )
 
-        nc.scalar.copy(out=dealt(w_first), in_=deal_source(0)[:, :, :, 0:2])
+        nc.scalar.copy(out=dealt(w_front[0]), in_=deal_source(0)[:, :, :, 0:2])
         quantize_x(2)
         quantize_x(3)
-        quantize_w(w_first[:].rearrange("p t c -> p (t c)"), 0, P)
-        nc.scalar.copy(out=dealt(w_dealt)[:, 0:HALF_M, :, 2:4], in_=deal_source(0)[:, :, :, 2:4])
-        nc.vector.tensor_copy(out=dealt(w_dealt)[:, HALF_M:], in_=deal_source(1))
+        quantize_w(w_front[0], 0, P)
+        nc.scalar.copy(out=dealt(w_back)[:, 0:HALF_M], in_=deal_source(0)[:, :, :, 2:4])
+        nc.vector.tensor_copy(out=dealt(w_front[1]), in_=deal_source(1)[:, :, :, 0:2])
+        nc.vector.tensor_copy(out=dealt(w_back)[:, HALF_M:], in_=deal_source(1)[:, :, :, 2:4])
+        quantize_w(w_front[1], P, 2 * P)
+        quantize_w(w_back, 2 * P, N)
         rest_sb = pool.tile([P, V], F32, name="rest_sb")
         nc.vector.tensor_scalar(rest_sb[:], frac_sb[:], -1.0, 1.0, MULT, ADD)
-        for t in range(2):
-            quantize_w(w_dealt[:, t, HALF_M * PACK :], P + t * HALF_M, P + (t + 1) * HALF_M)
-        quantize_w(w_dealt[:, 2:4, :].rearrange("p t c -> p (t c)"), 2 * P, N)
 
         y = [pool.tile([P, S], F32, name=f"y{t}") for t in range(PACK)]
 

@@ -61,23 +61,33 @@ def tile_picked_lerp_none_lo_kernel(
         identity = pool.tile([P, P], F32, name="identity")
         make_identity(nc, identity[:])
 
-        x_found = [{i: pool.tile([P, 2, P], F32, name=f"x_found{u}{i}") for i in (2, 3)} for u in range(2)]
-        x_picked = [pool.tile([P, P, PACK], BF16, name=f"x_picked{i}", align_bytes=64) for i in range(PACK)]
+        x_found = [pool.tile([P, 2, HALF_S], F32, name=f"x_found{u}") for u in range(2)]
+        x_woven = [pool.tile([P, HALF_S * PACK], BF16, name=f"x_woven{g}", align_bytes=64) for g in range(2)]
+        x_picked = [
+            x_woven[i // 2][:, i % 2 * P * PACK : (i % 2 + 1) * P * PACK].rearrange("p (s j) -> p s j", j=PACK)
+            for i in range(PACK)
+        ]
         x_codes = pool.tile([P, S], U32, name="x_codes", align_bytes=64)
         x_scales = pool.tile([P, S], U8, name="x_scales", align_bytes=64)
 
         def weave_views(u, i):
-            return x_picked[i][:, :, 2 * u : 2 * u + 2], x_found[u][i][:].rearrange("p j s -> p s j")
+            found = x_found[u][:, :, (i - 2) * P : (i - 1) * P]
+            return x_picked[i][:, :, 2 * u : 2 * u + 2], found.rearrange("p j s -> p s j")
 
-        def picked_by(j, i):
+        def picked_by(j, i, count=1):
             cols = P // 16
-            return x_raw[j][:].indirect(offs_sb[:, i * cols : (i + 1) * cols])
+            return x_raw[j][:].indirect(offs_sb[:, i * cols : (i + count) * cols])
 
         for j in range(PACK):
-            for i in (0, 1):
-                nc.vector.tensor_copy(out=x_picked[i][:, :, j], in_=picked_by(j, i))
-            for i in (2, 3):
-                nc.scalar.activation(x_found[j // 2][i][:, j % 2, :], picked_by(j, i), COPY)
+            if j < PACK - 1:
+                woven = x_woven[0][:].rearrange("p (s j) -> p s j", j=PACK)
+                nc.vector.tensor_copy(out=woven[:, :, j], in_=picked_by(j, 0, 2))
+                nc.scalar.activation(x_found[j // 2][:, j % 2, :], picked_by(j, 2, 2), COPY)
+            else:
+                for i in (0, 1):
+                    nc.vector.tensor_copy(out=x_picked[i][:, :, j], in_=picked_by(j, i))
+                for i in (2, 3):
+                    nc.scalar.activation(x_found[1][:, 1, (i - 2) * P : (i - 1) * P], picked_by(j, i), COPY)
             if j == 1:
                 nc.scalar.copy(*weave_views(0, 2))
                 nc.vector.tensor_copy(*weave_views(0, 3))
@@ -86,7 +96,7 @@ def tile_picked_lerp_none_lo_kernel(
             nc.vector.quantize_mx(
                 out=x_codes[:, i * P : (i + 1) * P].bitcast(FP8X4),
                 scales=x_scales[:, i * P : (i + 1) * P],
-                in_=x_picked[i][:].rearrange("p s j -> p (s j)"),
+                in_=x_woven[i // 2][:, i % 2 * P * PACK : (i % 2 + 1) * P * PACK],
             )
 
         nc.scalar.copy(*weave_views(1, 2))

@@ -22,6 +22,7 @@ PACK = 4
 HALF_S = S // 2
 HALF_N = N // 2
 HALF_M = P // 2
+QUARTER_M = P // 4
 HALF_V = V // 2
 
 
@@ -50,9 +51,9 @@ def tile_picked_lerp_none_lo_kernel(
             nc.sync.dma_start(out=x_raw[j][:], in_=x_rows[:, j, :])
         for h in range(2):
             nc.sync.dma_start(out=w_raw[h][:], in_=w_rows[:, :, h * HALF_N : (h + 1) * HALF_N])
+        nc.sync.dma_start(out=frac_sb[:], in_=frac)
         nc.sync.dma_start(right_sb[:], right)
         nc.sync.dma_start(left_sb[:], left)
-        nc.sync.dma_start(out=frac_sb[:], in_=frac)
 
         idle = pool.tile([P, 2], F32, name="idle")
         nc.gpsimd.memset(idle[:, 0:1], 0.0)
@@ -106,7 +107,8 @@ def tile_picked_lerp_none_lo_kernel(
 
         w_codes = pool.tile([P, N], U32, name="w_codes", align_bytes=64)
         w_scales = pool.tile([P, N], U8, name="w_scales", align_bytes=64)
-        w_front = [pool.tile([P, 2, HALF_M * PACK], BF16, name=f"w_front{h}", align_bytes=64) for h in range(2)]
+        w_first = [pool.tile([P, 2, QUARTER_M * PACK], BF16, name=f"w_first{u}", align_bytes=64) for u in range(2)]
+        w_second = pool.tile([P, 2, 2, QUARTER_M * PACK], BF16, name="w_second", align_bytes=64)
         w_back = pool.tile([P, 2, P * PACK], BF16, name="w_back", align_bytes=64)
 
         def deal_source(h):
@@ -122,17 +124,25 @@ def tile_picked_lerp_none_lo_kernel(
                 in_=tile[:].rearrange("p t c -> p (t c)"),
             )
 
-        nc.scalar.copy(out=dealt(w_front[0]), in_=deal_source(0)[:, :, :, 0:2])
+        for u in range(2):
+            nc.scalar.copy(out=dealt(w_first[u]), in_=deal_source(0)[:, u * QUARTER_M : (u + 1) * QUARTER_M, :, 0:2])
         quantize_x(2)
         quantize_x(3)
-        quantize_w(w_front[0], 0, P)
+        for u in range(2):
+            quantize_w(w_first[u], u * HALF_M, (u + 1) * HALF_M)
         nc.scalar.copy(out=dealt(w_back)[:, 0:HALF_M], in_=deal_source(0)[:, :, :, 2:4])
-        nc.vector.tensor_copy(out=dealt(w_front[1]), in_=deal_source(1)[:, :, :, 0:2])
+        nc.vector.tensor_copy(
+            out=w_second[:].rearrange("p u t (m j) -> p u m j t", j=PACK),
+            in_=w_raw[1][:].rearrange("p j (u m t) -> p u m j t", t=PACK, u=2)[:, :, :, :, 0:2],
+        )
         nc.vector.tensor_copy(out=dealt(w_back)[:, HALF_M:], in_=deal_source(1)[:, :, :, 2:4])
-        quantize_w(w_front[1], P, 2 * P)
+        nc.vector.quantize_mx(
+            out=w_codes[:, P : 2 * P].bitcast(FP8X4),
+            scales=w_scales[:, P : 2 * P],
+            in_=w_second[:].rearrange("p u t c -> p (u t c)"),
+        )
         quantize_w(w_back, 2 * P, N)
         rest_sb = pool.tile([P, V], F32, name="rest_sb")
-        nc.vector.tensor_scalar(rest_sb[:], frac_sb[:], -1.0, 1.0, MULT, ADD)
 
         y = [pool.tile([P, S], F32, name=f"y{t}") for t in range(PACK)]
 
@@ -153,6 +163,7 @@ def tile_picked_lerp_none_lo_kernel(
             product(0, first[i][:], slice(i * P, (i + 1) * P))
         for i in range(PACK):
             nc.scalar.copy(out=y[0][:, i * P : (i + 1) * P], in_=first[i][:])
+        nc.scalar.activation(rest_sb[:], frac_sb[:], COPY, bias=1.0, scale=-1.0)
         second = [psum.tile([P, HALF_S], F32, name=f"second{h}") for h in range(2)]
         acc = {t: psum.tile([P, S], F32, name=f"acc{t}") for t in (2, 3)}
         for h in range(2):
@@ -166,7 +177,8 @@ def tile_picked_lerp_none_lo_kernel(
 
         left_found = {t: pool.tile([P, V], F32, name=f"left_found{t}") for t in (2, 3)}
         left_part = [pool.tile([P, V], F32, name=f"left_part{t}") for t in range(PACK)]
-        right_part = [pool.tile([P, V], F32, name=f"right_part{t}") for t in range(PACK)]
+        reused = {1: "y0", 2: "y0"}
+        right_part = [pool.tile([P, V], F32, name=f"right_part{t}", tag=reused.get(t, f"right_part{t}")) for t in range(PACK)]
         result = pool.tile([P, PACK, V], F32, name="result")
         rounded = [pool.tile([P, HALF_V, PACK], BF16, name=f"rounded{h}", align_bytes=64) for h in range(2)]
         o_codes = pool.tile([P, V], U32, name="o_codes", align_bytes=64)
@@ -196,16 +208,16 @@ def tile_picked_lerp_none_lo_kernel(
         weigh_left(0)
         turn(0, right_part[0], start=True)
         turn(0, left_part[0])
-        weigh_right(1)
         weigh_left(1)
+        weigh_right(1)
         for t in (2, 3):
             nc.scalar.activation(left_found[t][:], y[t][:].indirect(left_sb[:]), COPY)
-        turn(1, right_part[1])
-        turn(1, left_part[1], stop=True)
+        turn(1, left_part[1])
+        turn(1, right_part[1], stop=True)
         for h in range(2):
             nc.scalar.copy(
-                out=regrouped[h][:].rearrange("p t (a m) -> p t a m", a=2),
-                in_=turned[h][:].rearrange("p a (t m) -> p t a m", t=2),
+                out=regrouped[h][:].rearrange("p t (a u m) -> p t a u m", a=2, u=2),
+                in_=turned[h][:].rearrange("p a (u t m) -> p t a u m", t=2, u=2),
             )
         summed = [psum.tile([P, 2, HALF_V], F32, name=f"summed{h}", tag=f"first{2 + h}") for h in range(2)]
         for h in range(2):

@@ -100,8 +100,10 @@ def tile_picked_lerp_none_lo_kernel(
                 in_=x_woven[i // 2][:, i % 2 * P * PACK : (i % 2 + 1) * P * PACK],
             )
 
-        nc.scalar.copy(*weave_views(1, 2))
+        woven, found = weave_views(1, 2)
+        nc.scalar.copy(woven[:, :HALF_M], found[:, :HALF_M])
         quantize_x(0)
+        nc.vector.tensor_copy(woven[:, HALF_M:], found[:, HALF_M:])
         nc.vector.tensor_copy(*weave_views(1, 3))
         quantize_x(1)
 

@@ -217,14 +217,18 @@ def tile_picked_lerp_none_lo_kernel(
         turn(1, left_part[1])
         turn(1, right_part[1], stop=True)
         for h in range(2):
-            nc.scalar.copy(
-                out=regrouped[h][:].rearrange("p t (a u m) -> p t a u m", a=2, u=2),
-                in_=turned[h][:].rearrange("p a (u t m) -> p t a u m", t=2, u=2),
-            )
-        summed = [psum.tile([P, 2, HALF_V], F32, name=f"summed{h}", tag=f"first{2 + h}") for h in range(2)]
+            for t in range(2):
+                nc.scalar.copy(
+                    out=regrouped[h][:, t, :].rearrange("p (a u m) -> p a u m", a=2, u=2),
+                    in_=turned[h][:].rearrange("p a (u t m) -> p t a u m", t=2, u=2)[:, t],
+                )
+        free_banks = [["first2", "first3"], ["second0", "second1"]]
+        summed = [
+            [psum.tile([P, HALF_V], F32, name=f"summed{h}{t}", tag=free_banks[h][t]) for t in range(2)] for h in range(2)
+        ]
         for h in range(2):
             for t in range(2):
-                nc.tensor.transpose(summed[h][:, t, :], regrouped[h][:, t, :], identity[:])
+                nc.tensor.transpose(summed[h][t][:], regrouped[h][:, t, :], identity[:])
         weigh_right(2)
         weigh_right(3)
         for t in (2, 3):
@@ -232,7 +236,8 @@ def tile_picked_lerp_none_lo_kernel(
         nc.vector.tensor_tensor(result[:, 2, :], left_part[2][:], right_part[2][:], ADD)
         nc.sync.dma_start(out=out_rows[:, 2, :], in_=result[:, 2, :])
         for h in range(2):
-            nc.scalar.copy(out=result[:, 0:2, v_cols(h)], in_=summed[h][:])
+            for t in range(2):
+                nc.scalar.copy(out=result[:, t, v_cols(h)], in_=summed[h][t][:])
         nc.sync.dma_start(out=out_rows[:, 0:2, :], in_=result[:, 0:2, :])
         for h in range(2):
             nc.vector.tensor_tensor(

from contextlib import ExitStack

import concourse.mybir as mybir
from concourse.masks import make_identity

K, T, S, V, N = 512, 1024, 512, 256, 512
FLOPS = 2 * K * N * S

F32 = mybir.dt.float32
BF16 = mybir.dt.bfloat16
I32 = mybir.dt.int32
U32 = mybir.dt.uint32
U16 = mybir.dt.uint16
U8 = mybir.dt.uint8
FP8X4 = mybir.dt.float8_e4m3fn_x4
MULT = mybir.AluOpType.mult
ADD = mybir.AluOpType.add
COPY = mybir.ActivationFunctionType.Copy

P = 128
PACK = 4
HALF_S = S // 2
HALF_N = N // 2
HALF_M = P // 2
QUARTER_M = P // 4
HALF_V = V // 2


def tile_picked_lerp_none_lo_kernel(
    tc, xT, w1, frac, offs, left, right, out_0, out_1, out_2
):
    nc = tc.nc
    with ExitStack() as ctx:
        lists = ctx.enter_context(tc.tile_pool(name="lists", bufs=1))
        pool = ctx.enter_context(tc.tile_pool(name="pool", bufs=1))
        psum = ctx.enter_context(tc.psum_pool(name="psum", bufs=1))

        offs_sb = lists.tile([P, S // 16], U16, name="offs_sb")
        left_sb = lists.tile([P, V // 16], U16, name="left_sb")
        right_sb = lists.tile([P, V // 16], U16, name="right_sb")

        x_rows = xT.rearrange("(p j) t -> p j t", j=PACK)
        w_rows = w1.rearrange("(p j) m -> p j m", j=PACK)
        x_raw = [pool.tile([P, T], F32, name=f"x_raw{j}") for j in range(PACK)]
        w_raw = [pool.tile([P, PACK, HALF_N], F32, name=f"w_raw{h}") for h in range(2)]
        frac_sb = pool.tile([P, V], F32, name="frac_sb")

        nc.sync.dma_start(out=x_raw[0][:], in_=x_rows[:, 0, :])
        nc.sync.dma_start(offs_sb[:], offs)
        for j in range(1, PACK):
            nc.sync.dma_start(out=x_raw[j][:], in_=x_rows[:, j, :])
        for h in range(2):
            nc.sync.dma_start(out=w_raw[h][:], in_=w_rows[:, :, h * HALF_N : (h + 1) * HALF_N])
        nc.sync.dma_start(out=frac_sb[:], in_=frac)
        nc.sync.dma_start(right_sb[:], right)
        nc.sync.dma_start(left_sb[:], left)

        idle = pool.tile([P, 2], F32, name="idle")
        nc.gpsimd.memset(idle[:, 0:1], 0.0)
        nc.scalar.copy(out=idle[:, 1:2], in_=idle[:, 0:1])

        identity = pool.tile([P, P], F32, name="identity")
        make_identity(nc, identity[:])

        x_found = [pool.tile([P, 2, HALF_S], F32, name=f"x_found{u}") for u in range(2)]
        x_woven = [pool.tile([P, HALF_S * PACK], BF16, name=f"x_woven{g}", align_bytes=64) for g in range(2)]
        x_picked = [
            x_woven[i // 2][:, i % 2 * P * PACK : (i % 2 + 1) * P * PACK].rearrange("p (s j) -> p s j", j=PACK)
            for i in range(PACK)
        ]
        x_codes = pool.tile([P, S], U32, name="x_codes", align_bytes=64)
        x_scales = pool.tile([P, S], U8, name="x_scales", align_bytes=64)

        def weave_views(u, i):
            found = x_found[u][:, :, (i - 2) * P : (i - 1) * P]
            return x_picked[i][:, :, 2 * u : 2 * u + 2], found.rearrange("p j s -> p s j")

        def picked_by(j, i, count=1):
            cols = P // 16
            return x_raw[j][:].indirect(offs_sb[:, i * cols : (i + count) * cols])

        for j in range(PACK):
            if j < PACK - 1:
                woven = x_woven[0][:].rearrange("p (s j) -> p s j", j=PACK)
                nc.vector.tensor_copy(out=woven[:, :, j], in_=picked_by(j, 0, 2))
                nc.scalar.activation(x_found[j // 2][:, j % 2, :], picked_by(j, 2, 2), COPY)
            else:
                for i in (0, 1):
                    nc.vector.tensor_copy(out=x_picked[i][:, :, j], in_=picked_by(j, i))
                for i in (2, 3):
                    nc.scalar.activation(x_found[1][:, 1, (i - 2) * P : (i - 1) * P], picked_by(j, i), COPY)
            if j == 1:
                nc.scalar.copy(*weave_views(0, 2))
                nc.vector.tensor_copy(*weave_views(0, 3))

        def quantize_x(i):
            nc.vector.quantize_mx(
                out=x_codes[:, i * P : (i + 1) * P].bitcast(FP8X4),
                scales=x_scales[:, i * P : (i + 1) * P],
                in_=x_woven[i // 2][:, i % 2 * P * PACK : (i % 2 + 1) * P * PACK],
            )

        woven, found = weave_views(1, 2)
        nc.scalar.copy(woven[:, :HALF_M], found[:, :HALF_M])
        quantize_x(0)
        nc.vector.tensor_copy(woven[:, HALF_M:], found[:, HALF_M:])
        nc.vector.tensor_copy(*weave_views(1, 3))
        quantize_x(1)

        w_codes = pool.tile([P, N], U32, name="w_codes", align_bytes=64)
        w_scales = pool.tile([P, N], U8, name="w_scales", align_bytes=64)
        w_first = [pool.tile([P, 2, QUARTER_M * PACK], BF16, name=f"w_first{u}", align_bytes=64) for u in range(2)]
        w_second = pool.tile([P, 2, 2, QUARTER_M * PACK], BF16, name="w_second", align_bytes=64)
        w_back = pool.tile([P, 2, P * PACK], BF16, name="w_back", align_bytes=64)

        def deal_source(h):
            return w_raw[h][:].rearrange("p j (m t) -> p m j t", t=PACK)

        def dealt(tile):
            return tile[:].rearrange("p t (m j) -> p m j t", j=PACK)

        def quantize_w(tile, c0, c1):
            nc.vector.quantize_mx(
                out=w_codes[:, c0:c1].bitcast(FP8X4),
                scales=w_scales[:, c0:c1],
                in_=tile[:].rearrange("p t c -> p (t c)"),
            )

        for u in range(2):
            nc.scalar.copy(out=dealt(w_first[u]), in_=deal_source(0)[:, u * QUARTER_M : (u + 1) * QUARTER_M, :, 0:2])
        quantize_x(2)
        quantize_x(3)
        for u in range(2):
            quantize_w(w_first[u], u * HALF_M, (u + 1) * HALF_M)
        nc.scalar.copy(out=dealt(w_back)[:, 0:HALF_M], in_=deal_source(0)[:, :, :, 2:4])
        nc.vector.tensor_copy(
            out=w_second[:].rearrange("p u t (m j) -> p u m j t", j=PACK),
            in_=w_raw[1][:].rearrange("p j (u m t) -> p u m j t", t=PACK, u=2)[:, :, :, :, 0:2],
        )
        nc.vector.tensor_copy(out=dealt(w_back)[:, HALF_M:], in_=deal_source(1)[:, :, :, 2:4])
        nc.vector.quantize_mx(
            out=w_codes[:, P : 2 * P].bitcast(FP8X4),
            scales=w_scales[:, P : 2 * P],
            in_=w_second[:].rearrange("p u t c -> p (u t c)"),
        )
        quantize_w(w_back, 2 * P, N)
        rest_sb = pool.tile([P, V], F32, name="rest_sb")

        y = [pool.tile([P, S], F32, name=f"y{t}") for t in range(PACK)]

        def product(t, acc, picked):
            rows = slice(t * P, (t + 1) * P)
            nc.tensor.matmul_mx(
                out=acc,
                lhsT=w_codes[:, rows].bitcast(FP8X4),
                lhsT_scale=w_scales[:, rows],
                rhs=x_codes[:, picked].bitcast(FP8X4),
                rhs_scale=x_scales[:, picked],
                start=True,
                stop=True,
            )

        first = [psum.tile([P, P], F32, name=f"first{i}") for i in range(PACK)]
        for i in range(PACK):
            product(0, first[i][:], slice(i * P, (i + 1) * P))
        for i in range(PACK):
            nc.scalar.copy(out=y[0][:, i * P : (i + 1) * P], in_=first[i][:])
        nc.scalar.activation(rest_sb[:], frac_sb[:], COPY, bias=1.0, scale=-1.0)
        second = [psum.tile([P, HALF_S], F32, name=f"second{h}") for h in range(2)]
        acc = {t: psum.tile([P, S], F32, name=f"acc{t}") for t in (2, 3)}
        for h in range(2):
            product(1, second[h][:], slice(h * HALF_S, (h + 1) * HALF_S))
        for t in acc:
            product(t, acc[t][:], slice(0, S))
        for h in range(2):
            nc.scalar.copy(out=y[1][:, h * HALF_S : (h + 1) * HALF_S], in_=second[h][:])
        for t in acc:
            nc.scalar.copy(out=y[t][:], in_=acc[t][:])

        left_found = {t: pool.tile([P, V], F32, name=f"left_found{t}") for t in (2, 3)}
        left_part = [pool.tile([P, V], F32, name=f"left_part{t}") for t in range(PACK)]
        reused = {1: "y0", 2: "y0"}
        right_part = [pool.tile([P, V], F32, name=f"right_part{t}", tag=reused.get(t, f"right_part{t}")) for t in range(PACK)]
        result = pool.tile([P, PACK, V], F32, name="result")
        rounded = [pool.tile([P, HALF_V, PACK], BF16, name=f"rounded{h}", align_bytes=64) for h in range(2)]
        o_codes = pool.tile([P, V], U32, name="o_codes", align_bytes=64)
        o_scales = pool.tile([P, V], U8, name="o_scales", align_bytes=64)
        out_rows = out_0.rearrange("(p t) v -> p t v", t=PACK)

        def v_cols(h):
            return slice(h * HALF_V, (h + 1) * HALF_V)

        regrouped = [pool.tile([P, 2, P], F32, name=f"regrouped{h}") for h in range(2)]

        def weigh_right(t):
            nc.vector.tensor_tensor(right_part[t][:], y[t][:].indirect(right_sb[:]), frac_sb[:], MULT)

        def weigh_left(t):
            nc.vector.tensor_tensor(left_part[t][:], y[t][:].indirect(left_sb[:]), rest_sb[:], MULT)

        turned = [psum.tile([P, 2, P], F32, name=f"turned{h}", tag=f"first{h}") for h in range(2)]

        def turn(a, part, start=False, stop=False):
            for h in range(2):
                nc.tensor.matmul(
                    turned[h][:, a, :], part[:, v_cols(h)], identity[:], start=start, stop=stop, is_transpose=True
                )

        weigh_right(0)
        weigh_left(0)
        turn(0, right_part[0], start=True)
        turn(0, left_part[0])
        weigh_left(1)
        weigh_right(1)
        for t in (2, 3):
            nc.scalar.activation(left_found[t][:], y[t][:].indirect(left_sb[:]), COPY)
        turn(1, left_part[1])
        turn(1, right_part[1], stop=True)
        for h in range(2):
            for t in range(2):
                nc.scalar.copy(
                    out=regrouped[h][:, t, :].rearrange("p (a u m) -> p a u m", a=2, u=2),
                    in_=turned[h][:].rearrange("p a (u t m) -> p t a u m", t=2, u=2)[:, t],
                )
        free_banks = [["first2", "first3"], ["second0", "second1"]]
        summed = [
            [psum.tile([P, HALF_V], F32, name=f"summed{h}{t}", tag=free_banks[h][t]) for t in range(2)] for h in range(2)
        ]
        for h in range(2):
            for t in range(2):
                nc.tensor.transpose(summed[h][t][:], regrouped[h][:, t, :], identity[:])
        weigh_right(2)
        weigh_right(3)
        for t in (2, 3):
            nc.vector.tensor_tensor(left_part[t][:], left_found[t][:], rest_sb[:], MULT)
        nc.vector.tensor_tensor(result[:, 2, :], left_part[2][:], right_part[2][:], ADD)
        nc.sync.dma_start(out=out_rows[:, 2, :], in_=result[:, 2, :])
        for h in range(2):
            for t in range(2):
                nc.scalar.copy(out=result[:, t, v_cols(h)], in_=summed[h][t][:])
        nc.sync.dma_start(out=out_rows[:, 0:2, :], in_=result[:, 0:2, :])
        for h in range(2):
            nc.vector.tensor_tensor(
                result[:, 3, v_cols(h)], left_part[3][:, v_cols(h)], right_part[3][:, v_cols(h)], ADD
            )
        nc.sync.dma_start(out=out_rows[:, 3, :], in_=result[:, 3, :])
        for h in range(2):
            nc.vector.tensor_copy(
                out=rounded[h][:].rearrange("p (c i) t -> p c t i", i=PACK),
                in_=result[:, :, v_cols(h)].rearrange("p t (c i) -> p c t i", i=PACK),
            )
        for h in range(2):
            nc.vector.quantize_mx(
                out=o_codes[:, v_cols(h)].bitcast(FP8X4),
                scales=o_scales[:, v_cols(h)],
                in_=rounded[h][:].rearrange("p v t -> p (v t)"),
            )

        nc.sync.dma_start(
            out=out_1.rearrange("z p c r -> p (z c r)").bitcast(I32), in_=o_codes[:].bitcast(I32)
        )
        for q in range(4):
            queue = nc.scalar if q % 2 == 0 else nc.sync
            queue.dma_start(
                out=out_2[0, 4 * q : 4 * q + 4, :].bitcast(I32), in_=o_scales[32 * q : 32 * q + 4, :].bitcast(I32)
            )
